import numpy as np
import ml_dtypes


def mxq(x, axis, fmt="e4m3"):
    dtype, down = {"e4m3": (ml_dtypes.float8_e4m3fn, 7), "e5m2": (ml_dtypes.float8_e5m2, 14)}[fmt]
    v = np.moveaxis(np.asarray(x, np.float32).astype(ml_dtypes.bfloat16).astype(np.float64), axis, -1)
    blocks = v.reshape(v.shape[:-1] + (-1, 32))
    amax = np.abs(blocks).max(-1, keepdims=True)
    byte = np.maximum(np.where(amax > 0, np.frexp(amax)[1] - 1 + 127, 0) - down, 1)
    scale = np.exp2(byte - 127.0)
    codes = (blocks / scale).astype(np.float32).astype(dtype).astype(np.float64)
    return np.moveaxis((codes * scale).reshape(v.shape), -1, axis)


WIDE = False


def mx_kscale(k):
    if not WIDE:
        return np.ones(k)
    levels = np.array([10, -10, 5, -5, 0])
    if k % 512:
        return np.exp2(np.random.permutation(np.resize(levels, k // 32))).repeat(32)
    a = np.empty((k // 512, 16))
    for p in range(k // 512):
        a[p, :8] = np.random.permutation(np.resize(levels, 8))
        for g in range(8):
            far = levels[np.abs(levels - a[p, g]) >= 10]
            a[p, g + 8] = far[np.random.randint(len(far))]
    return np.exp2(a.ravel()).repeat(32)


def f64(x):
    return np.asarray(x).astype(np.float64)


def striped(idx):
    return np.tile(idx.reshape(-1, 16).T, (8, 1)).astype(np.uint16)


def unstriped(offs):
    return offs[:16].T.reshape(-1).astype(np.int64)


K, T, D, S, V, N = 1536, 1024, 2, 512, 256, 128


def setup_inputs():
    n = np.random.standard_normal
    s = mx_kscale(K)[:, None]
    return {
        "xT": (n((K, T)) * s).astype(np.float32),
        "w": (n((D, K, N)) / np.sqrt(D * K) / s[None]).astype(np.float32),
        "gate": np.tile(np.random.uniform(0.2, 1.0, S), (N, 1)).astype(np.float32),
        "offs": striped(np.random.permutation(T)[:S]),
    }


def reference(xT, w, gate, offs):
    idx = unstriped(offs)
    xq = mxq(f64(xT)[:, idx], 0, "e4m3")
    wq = mxq(f64(w), 1, "e4m3")
    y = sum(wq[d].T @ xq[:, d * V:(d + 1) * V] for d in range(D))
    out = np.zeros((N, T))
    out[:, idx] = f64(gate) * np.tile(y, (1, D))
    return out

@@ -1,0 +1,202 @@
+from contextlib import ExitStack
+
+import concourse.mybir as mybir
+
+K, T, D, S, V, N = 1536, 1024, 2, 512, 256, 128
+FLOPS = 2 * K * D * V * N
+
+F32 = mybir.dt.float32
+BF16 = mybir.dt.bfloat16
+U32 = mybir.dt.uint32
+U16 = mybir.dt.uint16
+U8 = mybir.dt.uint8
+FP8X4 = mybir.dt.float8_e4m3fn_x4
+MULT = mybir.AluOpType.mult
+
+P = 128
+PACK = 4
+PASSES = K // (P * PACK)
+HALF = V // 2
+WHOLE = (True, False, False)
+STRETCHES = (
+    ((0, 512, 224), (512, 512, 224)),
+    ((0, 512, 384), (512, 512, 320)),
+    ((0, 512, 288), (512, 256, 256), (768, 256, 96)),
+)
+
+
+def interleave(dst, src):
+    return (
+        dst.rearrange("p (c i) t -> p c t i", i=4),
+        src.rearrange("p t (c i) -> p c t i", i=4),
+    )
+
+
+def tile_picked_tome_lin_none_sub_e_kernel(tc, xT, w, gate, offs, out):
+    nc = tc.nc
+    with ExitStack() as ctx:
+        held = ctx.enter_context(tc.tile_pool(name="held", bufs=1))
+        psum = ctx.enter_context(tc.psum_pool(name="psum", bufs=1))
+
+        offsets = held.tile([P, S // 16], U16, name="offsets")
+        window = held.tile([P, T], F32, name="window", align_bytes=64)
+        gates = held.tile([P, S], F32, name="gates", align_bytes=64)
+
+        scales = held.tile([P, T], U8, name="scales", align_bytes=64)
+        codes = [held.tile([P, T], U32, name=f"codes{a}", align_bytes=64) for a in range(PASSES)]
+        picked_codes = [held.tile([P, S], U32, name=f"picked_codes{a}", align_bytes=64) for a in range(PASSES - 1)]
+        last_codes, picked_scales = [], []
+        w_grouped = {}
+        w_codes = held.tile([P, D * PASSES, N], U32, name="w_codes", align_bytes=64)
+        w_scales = held.tile([P, D * PASSES, N], U8, name="w_scales", align_bytes=64)
+
+        raw = {}
+        for a in range(PASSES):
+            rows = xT[a * P * PACK : (a + 1) * P * PACK, :].rearrange("(p j) t -> p j t", j=PACK)
+            if WHOLE[a]:
+                tile = held.tile([P, PACK, T], F32, name=f"raw{a}", align_bytes=64)
+                nc.sync.dma_start(tile[:], rows)
+            for s, (t0, n, cut) in enumerate(STRETCHES[a]):
+                if WHOLE[a]:
+                    raw[a, s] = tile[:, :, t0 : t0 + n]
+                else:
+                    part = held.tile([P, PACK, n], F32, name=f"raw{a}_{s}", align_bytes=64)
+                    nc.sync.dma_start(part[:], rows[:, :, t0 : t0 + n])
+                    raw[a, s] = part[:]
+            if a == 0:
+                nc.sync.dma_start(offsets[:], offs)
+        w_rows = w.rearrange("d k m -> (d k) m").rearrange("(u p j) m -> p u j m", p=P, j=PACK)
+        w_raw = {}
+        for u0, u1 in ((0, 2), (2, 4), (4, 5), (5, 6)):
+            tile = held.tile([P, u1 - u0, PACK, N], F32, name=f"w_raw{u0}", align_bytes=64)
+            nc.sync.dma_start(tile[:], w_rows[:, u0:u1, :, :])
+            for u in range(u0, u1):
+                w_raw[u] = tile[:, u - u0, :, :]
+        nc.sync.dma_start(gates[:], gate)
+
+        nc.vector.memset(window[:], 0.0)
+        nc.gpsimd.memset(scales[:], 0)
+
+        grouped = {}
+
+        def cast(a, s):
+            t0, n, cut = STRETCHES[a][s]
+            grouped[a, s] = held.tile([P, n, PACK], BF16, name=f"grouped{a}_{s}", align_bytes=64)
+            if cut < n:
+                nc.vector.tensor_copy(*interleave(grouped[a, s][:, cut:, :], raw[a, s][:, :, cut:]))
+            if cut > 0:
+                nc.scalar.copy(*interleave(grouped[a, s][:, :cut, :], raw[a, s][:, :, :cut]))
+
+        def quantise(a, s):
+            t0, n, cut = STRETCHES[a][s]
+            nc.vector.quantize_mx(
+                out=codes[a][:, t0 : t0 + n].bitcast(FP8X4),
+                scales=scales[4 * a :, t0 : t0 + n],
+                in_=grouped[a, s][:].rearrange("p t j -> p (t j)"),
+            )
+
+        def pick_codes(a):
+            nc.vector.tensor_copy(picked_codes[a][:], codes[a][:].indirect(offsets[:]))
+
+        def entries(d, h):
+            return d * V + h * HALF, d * V + (h + 1) * HALF
+
+        def pick_half(picked, table, h):
+            for d in range(D):
+                e0, e1 = entries(d, h)
+                nc.vector.tensor_copy(
+                    picked[:, d * HALF : (d + 1) * HALF], table[:].indirect(offsets[:, e0 // 16 : e1 // 16])
+                )
+
+        def pick_last(h):
+            last_codes.append(held.tile([P, V], U32, name=f"last_codes{h}", tag=f"late_codes{h}", align_bytes=64))
+            picked_scales.append(held.tile([P, V], U8, name=f"picked_scales{h}", tag=f"late_scales{h}", align_bytes=64))
+            pick_half(picked_scales[h], scales, h)
+            pick_half(last_codes[h], codes[PASSES - 1], h)
+
+        def group_w(u0, u1, tag):
+            tile = held.tile([P, u1 - u0, N, PACK], BF16, name=f"w_grouped{u0}", tag=tag, align_bytes=64)
+            for u in range(u0, u1):
+                w_grouped[u] = tile[:, u - u0, :, :]
+            w_grouped[u0, u1] = tile[:].rearrange("p u m j -> p (u m j)")
+
+        def cast_w(u, copy):
+            copy(*interleave(w_grouped[u], w_raw[u]))
+
+        def cast_w_on_gpsimd(u):
+            nc.gpsimd.tensor_copy(w_grouped[u], w_raw[u].rearrange("p j m -> p m j"))
+
+        def quantise_w(u0, u1):
+            nc.vector.quantize_mx(
+                out=w_codes[:, u0:u1, :].rearrange("p u m -> p (u m)").bitcast(FP8X4),
+                scales=w_scales[:, u0:u1, :].rearrange("p u m -> p (u m)"),
+                in_=w_grouped[u0, u1],
+            )
+
+        def codes_of(a, d, h):
+            e0, e1 = entries(d, h)
+            if a < PASSES - 1:
+                return picked_codes[a][:, e0:e1]
+            return last_codes[h][:, d * HALF : (d + 1) * HALF]
+
+        def multiply(h):
+            acc = psum.tile([P, HALF], F32, name=f"acc{h}")
+            for u in range(D * PASSES):
+                d, a = divmod(u, PASSES)
+                nc.tensor.matmul_mx(
+                    out=acc[:],
+                    lhsT=w_codes[:, u, :].bitcast(FP8X4),
+                    lhsT_scale=w_scales[:, u, :],
+                    rhs=codes_of(a, d, h).bitcast(FP8X4),
+                    rhs_scale=picked_scales[h][4 * a :, d * HALF : (d + 1) * HALF],
+                    start=(u == 0),
+                    stop=(u == D * PASSES - 1),
+                )
+            y = held.tile([P, HALF], F32, name=f"y{h}", align_bytes=64)
+            nc.scalar.copy(y[:], acc[:])
+            return y
+
+        def put_back(y, h):
+            for d in range(D):
+                e0, e1 = entries(d, h)
+                nc.vector.tensor_tensor(
+                    window[:].indirect(offsets[:, e0 // 16 : e1 // 16]), y[:], gates[:, e0:e1], MULT
+                )
+
+        cast(0, 0)
+        cast(0, 1)
+        quantise(0, 0)
+        quantise(0, 1)
+        cast(1, 0)
+        pick_codes(0)
+        quantise(1, 0)
+        cast(1, 1)
+        quantise(1, 1)
+        cast(2, 0)
+        pick_codes(1)
+        quantise(2, 0)
+        cast(2, 1)
+        quantise(2, 1)
+        cast(2, 2)
+        quantise(2, 2)
+        group_w(0, 2, "w_grouped0")
+        group_w(2, 4, "w_grouped2")
+        group_w(4, 5, "late_codes1")
+        group_w(5, 6, "late_scales1")
+        cast_w(0, nc.scalar.copy)
+        cast_w(1, nc.scalar.copy)
+        cast_w(2, nc.scalar.copy)
+        cast_w(3, nc.scalar.copy)
+        cast_w(4, nc.scalar.copy)
+        pick_last(0)
+        quantise_w(0, 2)
+        quantise_w(2, 4)
+        cast_w(5, nc.vector.tensor_copy)
+        quantise_w(4, 5)
+        quantise_w(5, 6)
+        y0 = multiply(0)
+        pick_last(1)
+        y1 = multiply(1)
+        put_back(y0, 0)
+        put_back(y1, 1)
+        nc.sync.dma_start(out, window[:])

@@ -17,11 +17,11 @@ P = 128
 PACK = 4
 PASSES = K // (P * PACK)
 HALF = V // 2
-WHOLE = (True, False, False)
+WHOLE = (True, True, False)
 STRETCHES = (
-    ((0, 512, 224), (512, 512, 224)),
-    ((0, 512, 384), (512, 512, 320)),
-    ((0, 512, 288), (512, 256, 256), (768, 256, 96)),
+    ((0, 512, 64), (512, 512, 352)),
+    ((0, 512, 64), (512, 512, 352)),
+    ((0, 512, 384), (512, 256, 256), (768, 256, 96)),
 )
 
 
@@ -45,7 +45,9 @@ def tile_picked_tome_lin_none_sub_e_kernel(tc, xT, w, gate, offs, out):
         scales = held.tile([P, T], U8, name="scales", align_bytes=64)
         codes = [held.tile([P, T], U32, name=f"codes{a}", align_bytes=64) for a in range(PASSES)]
         picked_codes = [held.tile([P, S], U32, name=f"picked_codes{a}", align_bytes=64) for a in range(PASSES - 1)]
-        last_codes, picked_scales = [], []
+        last_codes = []
+        picked_scales = held.tile([P, S], U8, name="picked_scales", align_bytes=64)
+        results = held.tile([P, S - HALF], F32, name="results", align_bytes=64)
         w_grouped = {}
         w_codes = held.tile([P, D * PASSES, N], U32, name="w_codes", align_bytes=64)
         w_scales = held.tile([P, D * PASSES, N], U8, name="w_scales", align_bytes=64)
@@ -67,11 +69,10 @@ def tile_picked_tome_lin_none_sub_e_kernel(tc, xT, w, gate, offs, out):
                 nc.sync.dma_start(offsets[:], offs)
         w_rows = w.rearrange("d k m -> (d k) m").rearrange("(u p j) m -> p u j m", p=P, j=PACK)
         w_raw = {}
-        for u0, u1 in ((0, 2), (2, 4), (4, 5), (5, 6)):
-            tile = held.tile([P, u1 - u0, PACK, N], F32, name=f"w_raw{u0}", align_bytes=64)
-            nc.sync.dma_start(tile[:], w_rows[:, u0:u1, :, :])
-            for u in range(u0, u1):
-                w_raw[u] = tile[:, u - u0, :, :]
+        for u in range(D * PASSES):
+            tile = held.tile([P, PACK, N], F32, name=f"w_raw{u}", align_bytes=64)
+            nc.sync.dma_start(tile[:], w_rows[:, u, :, :])
+            w_raw[u] = tile[:]
         nc.sync.dma_start(gates[:], gate)
 
         nc.vector.memset(window[:], 0.0)
@@ -110,8 +111,6 @@ def tile_picked_tome_lin_none_sub_e_kernel(tc, xT, w, gate, offs, out):
 
         def pick_last(h):
             last_codes.append(held.tile([P, V], U32, name=f"last_codes{h}", tag=f"late_codes{h}", align_bytes=64))
-            picked_scales.append(held.tile([P, V], U8, name=f"picked_scales{h}", tag=f"late_scales{h}", align_bytes=64))
-            pick_half(picked_scales[h], scales, h)
             pick_half(last_codes[h], codes[PASSES - 1], h)
 
         def group_w(u0, u1, tag):
@@ -123,8 +122,9 @@ def tile_picked_tome_lin_none_sub_e_kernel(tc, xT, w, gate, offs, out):
         def cast_w(u, copy):
             copy(*interleave(w_grouped[u], w_raw[u]))
 
-        def cast_w_on_gpsimd(u):
-            nc.gpsimd.tensor_copy(w_grouped[u], w_raw[u].rearrange("p j m -> p m j"))
+        def cast_w_shared(u):
+            nc.scalar.copy(*interleave(w_grouped[u][:, : N // 2, :], w_raw[u][:, :, : N // 2]))
+            nc.vector.tensor_copy(*interleave(w_grouped[u][:, N // 2 :, :], w_raw[u][:, :, N // 2 :]))
 
         def quantise_w(u0, u1):
             nc.vector.quantize_mx(
@@ -148,55 +148,46 @@ def tile_picked_tome_lin_none_sub_e_kernel(tc, xT, w, gate, offs, out):
                     lhsT=w_codes[:, u, :].bitcast(FP8X4),
                     lhsT_scale=w_scales[:, u, :],
                     rhs=codes_of(a, d, h).bitcast(FP8X4),
-                    rhs_scale=picked_scales[h][4 * a :, d * HALF : (d + 1) * HALF],
+                    rhs_scale=picked_scales[4 * a :, entries(d, h)[0] : entries(d, h)[1]],
                     start=(u == 0),
                     stop=(u == D * PASSES - 1),
                 )
-            y = held.tile([P, HALF], F32, name=f"y{h}", align_bytes=64)
-            nc.scalar.copy(y[:], acc[:])
-            return y
+            for c0 in range((1 - h) * HALF, S - HALF, V):
+                nc.scalar.copy(results[:, c0 : c0 + HALF], acc[:])
 
-        def put_back(y, h):
-            for d in range(D):
-                e0, e1 = entries(d, h)
-                nc.vector.tensor_tensor(
-                    window[:].indirect(offsets[:, e0 // 16 : e1 // 16]), y[:], gates[:, e0:e1], MULT
-                )
+        def put_back(e0, e1, c0):
+            nc.vector.tensor_tensor(
+                window[:].indirect(offsets[:, e0 // 16 : e1 // 16]),
+                results[:, c0 : c0 + e1 - e0],
+                gates[:, e0:e1],
+                MULT,
+            )
 
-        cast(0, 0)
-        cast(0, 1)
-        quantise(0, 0)
-        quantise(0, 1)
-        cast(1, 0)
-        pick_codes(0)
-        quantise(1, 0)
-        cast(1, 1)
-        quantise(1, 1)
-        cast(2, 0)
-        pick_codes(1)
-        quantise(2, 0)
-        cast(2, 1)
-        quantise(2, 1)
-        cast(2, 2)
-        quantise(2, 2)
+        for a in range(PASSES):
+            for s in range(len(STRETCHES[a])):
+                cast(a, s)
+                quantise(a, s)
+            if a < PASSES - 1:
+                pick_codes(a)
+        nc.vector.tensor_copy(picked_scales[:], scales[:].indirect(offsets[:]))
+        pick_last(0)
         group_w(0, 2, "w_grouped0")
         group_w(2, 4, "w_grouped2")
-        group_w(4, 5, "late_codes1")
-        group_w(5, 6, "late_scales1")
+        group_w(4, 5, "w_grouped4")
+        group_w(5, 6, "late_codes1")
         cast_w(0, nc.scalar.copy)
         cast_w(1, nc.scalar.copy)
+        quantise_w(0, 2)
         cast_w(2, nc.scalar.copy)
         cast_w(3, nc.scalar.copy)
-        cast_w(4, nc.scalar.copy)
-        pick_last(0)
-        quantise_w(0, 2)
         quantise_w(2, 4)
-        cast_w(5, nc.vector.tensor_copy)
+        cast_w(4, nc.scalar.copy)
         quantise_w(4, 5)
+        cast_w_shared(5)
         quantise_w(5, 6)
-        y0 = multiply(0)
+        multiply(0)
         pick_last(1)
-        y1 = multiply(1)
-        put_back(y0, 0)
-        put_back(y1, 1)
+        multiply(1)
+        put_back(0, HALF, HALF)
+        put_back(HALF, S, 0)
         nc.sync.dma_start(out, window[:])

@@ -19,9 +19,9 @@ PASSES = K // (P * PACK)
 HALF = V // 2
 WHOLE = (True, True, False)
 STRETCHES = (
-    ((0, 512, 64), (512, 512, 352)),
-    ((0, 512, 64), (512, 512, 352)),
-    ((0, 512, 384), (512, 256, 256), (768, 256, 96)),
+    ((0, 512, 224), (512, 512, 192)),
+    ((0, 512, 224), (512, 512, 192)),
+    ((0, 512, 352), (512, 256, 256), (768, 256, 96)),
 )
 
 
@@ -139,9 +139,9 @@ def tile_picked_tome_lin_none_sub_e_kernel(tc, xT, w, gate, offs, out):
                 return picked_codes[a][:, e0:e1]
             return last_codes[h][:, d * HALF : (d + 1) * HALF]
 
-        def multiply(h):
+        def multiply(h, units):
             acc = psum.tile([P, HALF], F32, name=f"acc{h}")
-            for u in range(D * PASSES):
+            for u in units:
                 d, a = divmod(u, PASSES)
                 nc.tensor.matmul_mx(
                     out=acc[:],
@@ -149,8 +149,8 @@ def tile_picked_tome_lin_none_sub_e_kernel(tc, xT, w, gate, offs, out):
                     lhsT_scale=w_scales[:, u, :],
                     rhs=codes_of(a, d, h).bitcast(FP8X4),
                     rhs_scale=picked_scales[4 * a :, entries(d, h)[0] : entries(d, h)[1]],
-                    start=(u == 0),
-                    stop=(u == D * PASSES - 1),
+                    start=(u == units[0]),
+                    stop=(u == units[-1]),
                 )
             for c0 in range((1 - h) * HALF, S - HALF, V):
                 nc.scalar.copy(results[:, c0 : c0 + HALF], acc[:])
@@ -173,8 +173,8 @@ def tile_picked_tome_lin_none_sub_e_kernel(tc, xT, w, gate, offs, out):
         pick_last(0)
         group_w(0, 2, "w_grouped0")
         group_w(2, 4, "w_grouped2")
-        group_w(4, 5, "w_grouped4")
-        group_w(5, 6, "late_codes1")
+        group_w(4, 5, "late_codes1")
+        group_w(5, 6, "w_grouped5")
         cast_w(0, nc.scalar.copy)
         cast_w(1, nc.scalar.copy)
         quantise_w(0, 2)
@@ -185,9 +185,9 @@ def tile_picked_tome_lin_none_sub_e_kernel(tc, xT, w, gate, offs, out):
         quantise_w(4, 5)
         cast_w_shared(5)
         quantise_w(5, 6)
-        multiply(0)
+        multiply(0, (0, 1, 2, 3, 4, 5))
         pick_last(1)
-        multiply(1)
+        multiply(1, (0, 1, 3, 4, 2, 5))
         put_back(0, HALF, HALF)
         put_back(HALF, S, 0)
         nc.sync.dma_start(out, window[:])

@@ -17,11 +17,12 @@ P = 128
 PACK = 4
 PASSES = K // (P * PACK)
 HALF = V // 2
-WHOLE = (True, True, False)
+UNITS = ((0, 0), (0, 1), (1, 0), (1, 1), (0, 2), (1, 2))
+LOADS = (((0, 1024),), ((0, 1024),), ((0, 512), (512, 512)))
 STRETCHES = (
     ((0, 512, 224), (512, 512, 192)),
     ((0, 512, 224), (512, 512, 192)),
-    ((0, 512, 352), (512, 256, 256), (768, 256, 96)),
+    ((0, 512, 384), (512, 256, 0), (768, 256, 160)),
 )
 
 
@@ -46,7 +47,6 @@ def tile_picked_tome_lin_none_sub_e_kernel(tc, xT, w, gate, offs, out):
         codes = [held.tile([P, T], U32, name=f"codes{a}", align_bytes=64) for a in range(PASSES)]
         picked_codes = [held.tile([P, S], U32, name=f"picked_codes{a}", align_bytes=64) for a in range(PASSES - 1)]
         last_codes = []
-        picked_scales = held.tile([P, S], U8, name="picked_scales", align_bytes=64)
         results = held.tile([P, S - HALF], F32, name="results", align_bytes=64)
         w_grouped = {}
         w_codes = held.tile([P, D * PASSES, N], U32, name="w_codes", align_bytes=64)
@@ -55,23 +55,20 @@ def tile_picked_tome_lin_none_sub_e_kernel(tc, xT, w, gate, offs, out):
         raw = {}
         for a in range(PASSES):
             rows = xT[a * P * PACK : (a + 1) * P * PACK, :].rearrange("(p j) t -> p j t", j=PACK)
-            if WHOLE[a]:
-                tile = held.tile([P, PACK, T], F32, name=f"raw{a}", align_bytes=64)
-                nc.sync.dma_start(tile[:], rows)
-            for s, (t0, n, cut) in enumerate(STRETCHES[a]):
-                if WHOLE[a]:
-                    raw[a, s] = tile[:, :, t0 : t0 + n]
-                else:
-                    part = held.tile([P, PACK, n], F32, name=f"raw{a}_{s}", align_bytes=64)
-                    nc.sync.dma_start(part[:], rows[:, :, t0 : t0 + n])
-                    raw[a, s] = part[:]
+            for l0, ln in LOADS[a]:
+                tile = held.tile([P, PACK, ln], F32, name=f"raw{a}_{l0}", align_bytes=64)
+                nc.sync.dma_start(tile[:], rows[:, :, l0 : l0 + ln])
+                for s, (t0, n, cut) in enumerate(STRETCHES[a]):
+                    if l0 <= t0 < l0 + ln:
+                        raw[a, s] = tile[:, :, t0 - l0 : t0 - l0 + n]
             if a == 0:
                 nc.sync.dma_start(offsets[:], offs)
         w_rows = w.rearrange("d k m -> (d k) m").rearrange("(u p j) m -> p u j m", p=P, j=PACK)
         w_raw = {}
-        for u in range(D * PASSES):
-            tile = held.tile([P, PACK, N], F32, name=f"w_raw{u}", align_bytes=64)
-            nc.sync.dma_start(tile[:], w_rows[:, u, :, :])
+        for u, (d, a) in enumerate(UNITS):
+            tag = {0: "early_scales"}.get(u, f"w_raw{u}")
+            tile = held.tile([P, PACK, N], F32, name=f"w_raw{u}", tag=tag, align_bytes=64)
+            nc.sync.dma_start(tile[:], w_rows[:, d * PASSES + a, :, :])
             w_raw[u] = tile[:]
         nc.sync.dma_start(gates[:], gate)
 
@@ -139,18 +136,23 @@ def tile_picked_tome_lin_none_sub_e_kernel(tc, xT, w, gate, offs, out):
                 return picked_codes[a][:, e0:e1]
             return last_codes[h][:, d * HALF : (d + 1) * HALF]
 
-        def multiply(h, units):
+        def scales_of(a, d, h):
+            e0, e1 = entries(d, h)
+            if e1 <= S - HALF:
+                return early_scales[4 * a :, e0:e1]
+            return late_scales[4 * a :, :]
+
+        def multiply(h):
             acc = psum.tile([P, HALF], F32, name=f"acc{h}")
-            for u in units:
-                d, a = divmod(u, PASSES)
+            for u, (d, a) in enumerate(UNITS):
                 nc.tensor.matmul_mx(
                     out=acc[:],
                     lhsT=w_codes[:, u, :].bitcast(FP8X4),
                     lhsT_scale=w_scales[:, u, :],
                     rhs=codes_of(a, d, h).bitcast(FP8X4),
-                    rhs_scale=picked_scales[4 * a :, entries(d, h)[0] : entries(d, h)[1]],
-                    start=(u == units[0]),
-                    stop=(u == units[-1]),
+                    rhs_scale=scales_of(a, d, h),
+                    start=(u == 0),
+                    stop=(u == len(UNITS) - 1),
                 )
             for c0 in range((1 - h) * HALF, S - HALF, V):
                 nc.scalar.copy(results[:, c0 : c0 + HALF], acc[:])
@@ -169,25 +171,28 @@ def tile_picked_tome_lin_none_sub_e_kernel(tc, xT, w, gate, offs, out):
                 quantise(a, s)
             if a < PASSES - 1:
                 pick_codes(a)
-        nc.vector.tensor_copy(picked_scales[:], scales[:].indirect(offsets[:]))
-        pick_last(0)
-        group_w(0, 2, "w_grouped0")
-        group_w(2, 4, "w_grouped2")
-        group_w(4, 5, "late_codes1")
-        group_w(5, 6, "w_grouped5")
+        group_w(0, 1, "w_grouped0")
+        group_w(1, 3, "w_grouped1")
+        group_w(3, 5, "late_scales")
+        group_w(5, 6, "late_codes1")
         cast_w(0, nc.scalar.copy)
+        quantise_w(0, 1)
+        early_scales = held.tile([P, S - HALF], U8, name="early_scales", tag="early_scales", align_bytes=64)
+        nc.vector.tensor_copy(early_scales[:], scales[:].indirect(offsets[:, : (S - HALF) // 16]))
+        pick_last(0)
         cast_w(1, nc.scalar.copy)
-        quantise_w(0, 2)
         cast_w(2, nc.scalar.copy)
+        quantise_w(1, 3)
         cast_w(3, nc.scalar.copy)
-        quantise_w(2, 4)
         cast_w(4, nc.scalar.copy)
-        quantise_w(4, 5)
+        quantise_w(3, 5)
         cast_w_shared(5)
         quantise_w(5, 6)
-        multiply(0, (0, 1, 2, 3, 4, 5))
+        multiply(0)
+        late_scales = held.tile([P, HALF], U8, name="late_scales", tag="late_scales", align_bytes=64)
+        nc.vector.tensor_copy(late_scales[:], scales[:].indirect(offsets[:, (S - HALF) // 16 :]))
         pick_last(1)
-        multiply(1, (0, 1, 3, 4, 2, 5))
+        multiply(1)
         put_back(0, HALF, HALF)
         put_back(HALF, S, 0)
         nc.sync.dma_start(out, window[:])

@@ -28,8 +28,8 @@ STRETCHES = (
 
 def interleave(dst, src):
     return (
-        dst.rearrange("p (c i) t -> p c t i", i=4),
-        src.rearrange("p t (c i) -> p c t i", i=4),
+        dst.rearrange("p (c i) t -> p c t i", i=2),
+        src.rearrange("p t (c i) -> p c t i", i=2),
     )
 
 

@@ -40,23 +40,23 @@ def tile_picked_tome_lin_none_sub_e_kernel(tc, xT, w, gate, offs, out):
         psum = ctx.enter_context(tc.psum_pool(name="psum", bufs=1))
 
         offsets = held.tile([P, S // 16], U16, name="offsets")
-        window = held.tile([P, T], F32, name="window", align_bytes=64)
-        gates = held.tile([P, S], F32, name="gates", align_bytes=64)
+        window = held.tile([P, T], F32, name="window", align_bytes=256)
+        gates = held.tile([P, S], F32, name="gates", align_bytes=256)
 
-        scales = held.tile([P, T], U8, name="scales", align_bytes=64)
-        codes = [held.tile([P, T], U32, name=f"codes{a}", align_bytes=64) for a in range(PASSES)]
-        picked_codes = [held.tile([P, S], U32, name=f"picked_codes{a}", align_bytes=64) for a in range(PASSES - 1)]
+        scales = held.tile([P, T], U8, name="scales", align_bytes=256)
+        codes = [held.tile([P, T], U32, name=f"codes{a}", align_bytes=256) for a in range(PASSES)]
+        picked_codes = [held.tile([P, S], U32, name=f"picked_codes{a}", align_bytes=256) for a in range(PASSES - 1)]
         last_codes = []
-        results = held.tile([P, S - HALF], F32, name="results", align_bytes=64)
+        results = held.tile([P, S - HALF], F32, name="results", align_bytes=256)
         w_grouped = {}
-        w_codes = held.tile([P, D * PASSES, N], U32, name="w_codes", align_bytes=64)
-        w_scales = held.tile([P, D * PASSES, N], U8, name="w_scales", align_bytes=64)
+        w_codes = held.tile([P, D * PASSES, N], U32, name="w_codes", align_bytes=256)
+        w_scales = held.tile([P, D * PASSES, N], U8, name="w_scales", align_bytes=256)
 
         raw = {}
         for a in range(PASSES):
             rows = xT[a * P * PACK : (a + 1) * P * PACK, :].rearrange("(p j) t -> p j t", j=PACK)
             for l0, ln in LOADS[a]:
-                tile = held.tile([P, PACK, ln], F32, name=f"raw{a}_{l0}", align_bytes=64)
+                tile = held.tile([P, PACK, ln], F32, name=f"raw{a}_{l0}", align_bytes=256)
                 nc.sync.dma_start(tile[:], rows[:, :, l0 : l0 + ln])
                 for s, (t0, n, cut) in enumerate(STRETCHES[a]):
                     if l0 <= t0 < l0 + ln:
@@ -67,7 +67,7 @@ def tile_picked_tome_lin_none_sub_e_kernel(tc, xT, w, gate, offs, out):
         w_raw = {}
         for u, (d, a) in enumerate(UNITS):
             tag = {0: "early_scales"}.get(u, f"w_raw{u}")
-            tile = held.tile([P, PACK, N], F32, name=f"w_raw{u}", tag=tag, align_bytes=64)
+            tile = held.tile([P, PACK, N], F32, name=f"w_raw{u}", tag=tag, align_bytes=256)
             nc.sync.dma_start(tile[:], w_rows[:, d * PASSES + a, :, :])
             w_raw[u] = tile[:]
         nc.sync.dma_start(gates[:], gate)
@@ -79,7 +79,7 @@ def tile_picked_tome_lin_none_sub_e_kernel(tc, xT, w, gate, offs, out):
 
         def cast(a, s):
             t0, n, cut = STRETCHES[a][s]
-            grouped[a, s] = held.tile([P, n, PACK], BF16, name=f"grouped{a}_{s}", align_bytes=64)
+            grouped[a, s] = held.tile([P, n, PACK], BF16, name=f"grouped{a}_{s}", align_bytes=256)
             if cut < n:
                 nc.vector.tensor_copy(*interleave(grouped[a, s][:, cut:, :], raw[a, s][:, :, cut:]))
             if cut > 0:
@@ -107,11 +107,11 @@ def tile_picked_tome_lin_none_sub_e_kernel(tc, xT, w, gate, offs, out):
                 )
 
         def pick_last(h):
-            last_codes.append(held.tile([P, V], U32, name=f"last_codes{h}", tag=f"late_codes{h}", align_bytes=64))
+            last_codes.append(held.tile([P, V], U32, name=f"last_codes{h}", tag=f"late_codes{h}", align_bytes=256))
             pick_half(last_codes[h], codes[PASSES - 1], h)
 
         def group_w(u0, u1, tag):
-            tile = held.tile([P, u1 - u0, N, PACK], BF16, name=f"w_grouped{u0}", tag=tag, align_bytes=64)
+            tile = held.tile([P, u1 - u0, N, PACK], BF16, name=f"w_grouped{u0}", tag=tag, align_bytes=256)
             for u in range(u0, u1):
                 w_grouped[u] = tile[:, u - u0, :, :]
             w_grouped[u0, u1] = tile[:].rearrange("p u m j -> p (u m j)")
@@ -177,7 +177,7 @@ def tile_picked_tome_lin_none_sub_e_kernel(tc, xT, w, gate, offs, out):
         group_w(5, 6, "late_codes1")
         cast_w(0, nc.scalar.copy)
         quantise_w(0, 1)
-        early_scales = held.tile([P, S - HALF], U8, name="early_scales", tag="early_scales", align_bytes=64)
+        early_scales = held.tile([P, S - HALF], U8, name="early_scales", tag="early_scales", align_bytes=256)
         nc.vector.tensor_copy(early_scales[:], scales[:].indirect(offsets[:, : (S - HALF) // 16]))
         pick_last(0)
         cast_w(1, nc.scalar.copy)
@@ -189,7 +189,7 @@ def tile_picked_tome_lin_none_sub_e_kernel(tc, xT, w, gate, offs, out):
         cast_w_shared(5)
         quantise_w(5, 6)
         multiply(0)
-        late_scales = held.tile([P, HALF], U8, name="late_scales", tag="late_scales", align_bytes=64)
+        late_scales = held.tile([P, HALF], U8, name="late_scales", tag="late_scales", align_bytes=256)
         nc.vector.tensor_copy(late_scales[:], scales[:].indirect(offsets[:, (S - HALF) // 16 :]))
         pick_last(1)
         multiply(1)

@@ -18,11 +18,11 @@ PACK = 4
 PASSES = K // (P * PACK)
 HALF = V // 2
 UNITS = ((0, 0), (0, 1), (1, 0), (1, 1), (0, 2), (1, 2))
-LOADS = (((0, 1024),), ((0, 1024),), ((0, 512), (512, 512)))
+LOADS = (((0, 1024),), ((0, 1024),), ((0, 512), (512, 256), (768, 256)))
 STRETCHES = (
     ((0, 512, 224), (512, 512, 192)),
     ((0, 512, 224), (512, 512, 192)),
-    ((0, 512, 384), (512, 256, 0), (768, 256, 160)),
+    ((0, 512, 320), (512, 256, 256), (768, 256, 96)),
 )
 
 
@@ -66,8 +66,7 @@ def tile_picked_tome_lin_none_sub_e_kernel(tc, xT, w, gate, offs, out):
         w_rows = w.rearrange("d k m -> (d k) m").rearrange("(u p j) m -> p u j m", p=P, j=PACK)
         w_raw = {}
         for u, (d, a) in enumerate(UNITS):
-            tag = {0: "early_scales"}.get(u, f"w_raw{u}")
-            tile = held.tile([P, PACK, N], F32, name=f"w_raw{u}", tag=tag, align_bytes=256)
+            tile = held.tile([P, PACK, N], F32, name=f"w_raw{u}", align_bytes=256)
             nc.sync.dma_start(tile[:], w_rows[:, d * PASSES + a, :, :])
             w_raw[u] = tile[:]
         nc.sync.dma_start(gates[:], gate)

@@ -17,11 +17,12 @@ P = 128
 PACK = 4
 PASSES = K // (P * PACK)
 HALF = V // 2
+W_CUT = 64
 UNITS = ((0, 0), (0, 1), (1, 0), (1, 1), (0, 2), (1, 2))
 LOADS = (((0, 1024),), ((0, 1024),), ((0, 512), (512, 256), (768, 256)))
 STRETCHES = (
-    ((0, 512, 224), (512, 512, 192)),
-    ((0, 512, 224), (512, 512, 192)),
+    ((0, 512, 96), (512, 256, 256), (768, 256, 64)),
+    ((0, 512, 96), (512, 256, 256), (768, 256, 64)),
     ((0, 512, 320), (512, 256, 256), (768, 256, 96)),
 )
 
@@ -119,8 +120,8 @@ def tile_picked_tome_lin_none_sub_e_kernel(tc, xT, w, gate, offs, out):
             copy(*interleave(w_grouped[u], w_raw[u]))
 
         def cast_w_shared(u):
-            nc.scalar.copy(*interleave(w_grouped[u][:, : N // 2, :], w_raw[u][:, :, : N // 2]))
-            nc.vector.tensor_copy(*interleave(w_grouped[u][:, N // 2 :, :], w_raw[u][:, :, N // 2 :]))
+            nc.scalar.copy(*interleave(w_grouped[u][:, :W_CUT, :], w_raw[u][:, :, :W_CUT]))
+            nc.vector.tensor_copy(*interleave(w_grouped[u][:, W_CUT:, :], w_raw[u][:, :, W_CUT:]))
 
         def quantise_w(u0, u1):
             nc.vector.quantize_mx(

@@ -17,7 +17,6 @@ P = 128
 PACK = 4
 PASSES = K // (P * PACK)
 HALF = V // 2
-W_CUT = 64
 UNITS = ((0, 0), (0, 1), (1, 0), (1, 1), (0, 2), (1, 2))
 LOADS = (((0, 1024),), ((0, 1024),), ((0, 512), (512, 256), (768, 256)))
 STRETCHES = (
@@ -67,7 +66,7 @@ def tile_picked_tome_lin_none_sub_e_kernel(tc, xT, w, gate, offs, out):
         w_rows = w.rearrange("d k m -> (d k) m").rearrange("(u p j) m -> p u j m", p=P, j=PACK)
         w_raw = {}
         for u, (d, a) in enumerate(UNITS):
-            tile = held.tile([P, PACK, N], F32, name=f"w_raw{u}", align_bytes=256)
+            tile = held.tile([P, PACK, N], F32, name=f"w_raw{u}", tag=f"w_raw{u}", align_bytes=256)
             nc.sync.dma_start(tile[:], w_rows[:, d * PASSES + a, :, :])
             w_raw[u] = tile[:]
         nc.sync.dma_start(gates[:], gate)
@@ -119,10 +118,6 @@ def tile_picked_tome_lin_none_sub_e_kernel(tc, xT, w, gate, offs, out):
         def cast_w(u, copy):
             copy(*interleave(w_grouped[u], w_raw[u]))
 
-        def cast_w_shared(u):
-            nc.scalar.copy(*interleave(w_grouped[u][:, :W_CUT, :], w_raw[u][:, :, :W_CUT]))
-            nc.vector.tensor_copy(*interleave(w_grouped[u][:, W_CUT:, :], w_raw[u][:, :, W_CUT:]))
-
         def quantise_w(u0, u1):
             nc.vector.quantize_mx(
                 out=w_codes[:, u0:u1, :].rearrange("p u m -> p (u m)").bitcast(FP8X4),
@@ -173,7 +168,7 @@ def tile_picked_tome_lin_none_sub_e_kernel(tc, xT, w, gate, offs, out):
                 pick_codes(a)
         group_w(0, 1, "w_grouped0")
         group_w(1, 3, "w_grouped1")
-        group_w(3, 5, "late_scales")
+        group_w(3, 5, "w_grouped3")
         group_w(5, 6, "late_codes1")
         cast_w(0, nc.scalar.copy)
         quantise_w(0, 1)
@@ -186,10 +181,10 @@ def tile_picked_tome_lin_none_sub_e_kernel(tc, xT, w, gate, offs, out):
         cast_w(3, nc.scalar.copy)
         cast_w(4, nc.scalar.copy)
         quantise_w(3, 5)
-        cast_w_shared(5)
+        cast_w(5, nc.scalar.copy)
         quantise_w(5, 6)
         multiply(0)
-        late_scales = held.tile([P, HALF], U8, name="late_scales", tag="late_scales", align_bytes=256)
+        late_scales = held.tile([P, HALF], U8, name="late_scales", tag="w_raw5", align_bytes=256)
         nc.vector.tensor_copy(late_scales[:], scales[:].indirect(offsets[:, (S - HALF) // 16 :]))
         pick_last(1)
         multiply(1)

@@ -170,7 +170,8 @@ def tile_picked_tome_lin_none_sub_e_kernel(tc, xT, w, gate, offs, out):
         group_w(1, 3, "w_grouped1")
         group_w(3, 5, "w_grouped3")
         group_w(5, 6, "late_codes1")
-        cast_w(0, nc.scalar.copy)
+        nc.vector.tensor_copy(*interleave(w_grouped[0][:, N // 2 :, :], w_raw[0][:, :, N // 2 :]))
+        nc.scalar.copy(*interleave(w_grouped[0][:, : N // 2, :], w_raw[0][:, :, : N // 2]))
         quantise_w(0, 1)
         early_scales = held.tile([P, S - HALF], U8, name="early_scales", tag="early_scales", align_bytes=256)
         nc.vector.tensor_copy(early_scales[:], scales[:].indirect(offsets[:, : (S - HALF) // 16]))

@@ -12,18 +12,17 @@ U16 = mybir.dt.uint16
 U8 = mybir.dt.uint8
 FP8X4 = mybir.dt.float8_e4m3fn_x4
 MULT = mybir.AluOpType.mult
+ADD = mybir.AluOpType.add
+COPY = mybir.ActivationFunctionType.Copy
 
 P = 128
 PACK = 4
 PASSES = K // (P * PACK)
-HALF = V // 2
-UNITS = ((0, 0), (0, 1), (1, 0), (1, 1), (0, 2), (1, 2))
-LOADS = (((0, 1024),), ((0, 1024),), ((0, 512), (512, 256), (768, 256)))
-STRETCHES = (
-    ((0, 512, 96), (512, 256, 256), (768, 256, 64)),
-    ((0, 512, 96), (512, 256, 256), (768, 256, 64)),
-    ((0, 512, 320), (512, 256, 256), (768, 256, 96)),
-)
+X_LOADS = (((0, 2), (2, 4)), ((0, 2), (2, 4)), ((0, 2), (2, 3), (3, 4)))
+SCALAR_ENTRIES = ((512, 512, 512, 0), (512, 512, 512, 0), (512, 512, 0, 256))
+W_LOADS = ((0, 2), (2, 4), (4, 5), (5, 6))
+VECTOR_CASTS = (5,)
+STORES = ((0, 512), (512, 1024))
 
 
 def interleave(dst, src):
@@ -40,155 +39,85 @@ def tile_picked_tome_lin_none_sub_e_kernel(tc, xT, w, gate, offs, out):
         psum = ctx.enter_context(tc.psum_pool(name="psum", bufs=1))
 
         offsets = held.tile([P, S // 16], U16, name="offsets")
-        window = held.tile([P, T], F32, name="window", align_bytes=256)
+        windows = [held.tile([P, T], F32, name=f"window{d}", align_bytes=256) for d in range(D)]
         gates = held.tile([P, S], F32, name="gates", align_bytes=256)
 
-        scales = held.tile([P, T], U8, name="scales", align_bytes=256)
-        codes = [held.tile([P, T], U32, name=f"codes{a}", align_bytes=256) for a in range(PASSES)]
-        picked_codes = [held.tile([P, S], U32, name=f"picked_codes{a}", align_bytes=256) for a in range(PASSES - 1)]
-        last_codes = []
-        results = held.tile([P, S - HALF], F32, name="results", align_bytes=256)
-        w_grouped = {}
-        w_codes = held.tile([P, D * PASSES, N], U32, name="w_codes", align_bytes=256)
-        w_scales = held.tile([P, D * PASSES, N], U8, name="w_scales", align_bytes=256)
-
-        raw = {}
+        planes = {}
         for a in range(PASSES):
             rows = xT[a * P * PACK : (a + 1) * P * PACK, :].rearrange("(p j) t -> p j t", j=PACK)
-            for l0, ln in LOADS[a]:
-                tile = held.tile([P, PACK, ln], F32, name=f"raw{a}_{l0}", align_bytes=256)
-                nc.sync.dma_start(tile[:], rows[:, :, l0 : l0 + ln])
-                for s, (t0, n, cut) in enumerate(STRETCHES[a]):
-                    if l0 <= t0 < l0 + ln:
-                        raw[a, s] = tile[:, :, t0 - l0 : t0 - l0 + n]
-            if a == 0:
-                nc.sync.dma_start(offsets[:], offs)
+            for j0, j1 in X_LOADS[a]:
+                tile = held.tile([P, j1 - j0, T], F32, name=f"raw{a}_{j0}", align_bytes=256)
+                nc.sync.dma_start(tile[:], rows[:, j0:j1, :])
+                for j in range(j0, j1):
+                    planes[a, j] = tile[:, j - j0, :]
+                if (a, j0) == (0, 0):
+                    nc.sync.dma_start(offsets[:], offs)
         w_rows = w.rearrange("d k m -> (d k) m").rearrange("(u p j) m -> p u j m", p=P, j=PACK)
         w_raw = {}
-        for u, (d, a) in enumerate(UNITS):
-            tile = held.tile([P, PACK, N], F32, name=f"w_raw{u}", tag=f"w_raw{u}", align_bytes=256)
-            nc.sync.dma_start(tile[:], w_rows[:, d * PASSES + a, :, :])
-            w_raw[u] = tile[:]
+        for u0, u1 in W_LOADS:
+            tile = held.tile([P, u1 - u0, PACK, N], F32, name=f"w_raw{u0}", align_bytes=256)
+            nc.sync.dma_start(tile[:], w_rows[:, u0:u1, :, :])
+            for u in range(u0, u1):
+                w_raw[u] = tile[:, u - u0, :, :]
         nc.sync.dma_start(gates[:], gate)
 
-        nc.vector.memset(window[:], 0.0)
-        nc.gpsimd.memset(scales[:], 0)
+        nc.gpsimd.memset(windows[1][:], 0.0)
+        nc.scalar.copy(windows[0][:], windows[1][:])
 
-        grouped = {}
-
-        def cast(a, s):
-            t0, n, cut = STRETCHES[a][s]
-            grouped[a, s] = held.tile([P, n, PACK], BF16, name=f"grouped{a}_{s}", align_bytes=256)
-            if cut < n:
-                nc.vector.tensor_copy(*interleave(grouped[a, s][:, cut:, :], raw[a, s][:, :, cut:]))
-            if cut > 0:
-                nc.scalar.copy(*interleave(grouped[a, s][:, :cut, :], raw[a, s][:, :, :cut]))
-
-        def quantise(a, s):
-            t0, n, cut = STRETCHES[a][s]
-            nc.vector.quantize_mx(
-                out=codes[a][:, t0 : t0 + n].bitcast(FP8X4),
-                scales=scales[4 * a :, t0 : t0 + n],
-                in_=grouped[a, s][:].rearrange("p t j -> p (t j)"),
-            )
-
-        def pick_codes(a):
-            nc.vector.tensor_copy(picked_codes[a][:], codes[a][:].indirect(offsets[:]))
-
-        def entries(d, h):
-            return d * V + h * HALF, d * V + (h + 1) * HALF
-
-        def pick_half(picked, table, h):
+        codes, scales = {}, {}
+        for a in range(PASSES):
+            picked = held.tile([P, PACK, S], F32, name=f"picked{a}", align_bytes=256)
+            for j in range(PACK):
+                cut = SCALAR_ENTRIES[a][j]
+                if cut > 0:
+                    nc.scalar.activation(picked[:, j, :cut], planes[a, j].indirect(offsets[:, : cut // 16]), COPY)
+                if cut < S:
+                    nc.vector.tensor_copy(picked[:, j, cut:], planes[a, j].indirect(offsets[:, cut // 16 :]))
+            grouped = {}
             for d in range(D):
-                e0, e1 = entries(d, h)
-                nc.vector.tensor_copy(
-                    picked[:, d * HALF : (d + 1) * HALF], table[:].indirect(offsets[:, e0 // 16 : e1 // 16])
+                grouped[d] = held.tile([P, V, PACK], BF16, name=f"grouped{a}_{d}", align_bytes=256)
+                nc.vector.tensor_copy(*interleave(grouped[d][:], picked[:, :, d * V : (d + 1) * V]))
+            for d in range(D):
+                codes[a, d] = held.tile([P, V], U32, name=f"codes{a}_{d}", align_bytes=256)
+                scales[a, d] = held.tile([P, V], U8, name=f"scales{a}_{d}", align_bytes=256)
+                nc.vector.quantize_mx(
+                    out=codes[a, d][:].bitcast(FP8X4),
+                    scales=scales[a, d][:],
+                    in_=grouped[d][:].rearrange("p t j -> p (t j)"),
                 )
 
-        def pick_last(h):
-            last_codes.append(held.tile([P, V], U32, name=f"last_codes{h}", tag=f"late_codes{h}", align_bytes=256))
-            pick_half(last_codes[h], codes[PASSES - 1], h)
-
-        def group_w(u0, u1, tag):
-            tile = held.tile([P, u1 - u0, N, PACK], BF16, name=f"w_grouped{u0}", tag=tag, align_bytes=256)
+        acc = psum.tile([P, V], F32, name="acc")
+        for u0, u1 in W_LOADS:
+            w_grouped = held.tile([P, u1 - u0, N, PACK], BF16, name=f"w_grouped{u0}", align_bytes=256)
+            w_codes = held.tile([P, (u1 - u0) * N], U32, name=f"w_codes{u0}", align_bytes=256)
+            w_scales = held.tile([P, (u1 - u0) * N], U8, name=f"w_scales{u0}", align_bytes=256)
             for u in range(u0, u1):
-                w_grouped[u] = tile[:, u - u0, :, :]
-            w_grouped[u0, u1] = tile[:].rearrange("p u m j -> p (u m j)")
-
-        def cast_w(u, copy):
-            copy(*interleave(w_grouped[u], w_raw[u]))
-
-        def quantise_w(u0, u1):
+                copy = nc.vector.tensor_copy if u in VECTOR_CASTS else nc.scalar.copy
+                copy(*interleave(w_grouped[:, u - u0, :, :], w_raw[u]))
             nc.vector.quantize_mx(
-                out=w_codes[:, u0:u1, :].rearrange("p u m -> p (u m)").bitcast(FP8X4),
-                scales=w_scales[:, u0:u1, :].rearrange("p u m -> p (u m)"),
-                in_=w_grouped[u0, u1],
+                out=w_codes[:].bitcast(FP8X4),
+                scales=w_scales[:],
+                in_=w_grouped[:].rearrange("p u m j -> p (u m j)"),
             )
-
-        def codes_of(a, d, h):
-            e0, e1 = entries(d, h)
-            if a < PASSES - 1:
-                return picked_codes[a][:, e0:e1]
-            return last_codes[h][:, d * HALF : (d + 1) * HALF]
-
-        def scales_of(a, d, h):
-            e0, e1 = entries(d, h)
-            if e1 <= S - HALF:
-                return early_scales[4 * a :, e0:e1]
-            return late_scales[4 * a :, :]
-
-        def multiply(h):
-            acc = psum.tile([P, HALF], F32, name=f"acc{h}")
-            for u, (d, a) in enumerate(UNITS):
+            for u in range(u0, u1):
+                d, a = divmod(u, PASSES)
+                cols = slice((u - u0) * N, (u - u0 + 1) * N)
                 nc.tensor.matmul_mx(
                     out=acc[:],
-                    lhsT=w_codes[:, u, :].bitcast(FP8X4),
-                    lhsT_scale=w_scales[:, u, :],
-                    rhs=codes_of(a, d, h).bitcast(FP8X4),
-                    rhs_scale=scales_of(a, d, h),
+                    lhsT=w_codes[:, cols].bitcast(FP8X4),
+                    lhsT_scale=w_scales[:, cols],
+                    rhs=codes[a, d][:].bitcast(FP8X4),
+                    rhs_scale=scales[a, d][:],
                     start=(u == 0),
-                    stop=(u == len(UNITS) - 1),
+                    stop=(u == D * PASSES - 1),
                 )
-            for c0 in range((1 - h) * HALF, S - HALF, V):
-                nc.scalar.copy(results[:, c0 : c0 + HALF], acc[:])
 
-        def put_back(e0, e1, c0):
-            nc.vector.tensor_tensor(
-                window[:].indirect(offsets[:, e0 // 16 : e1 // 16]),
-                results[:, c0 : c0 + e1 - e0],
-                gates[:, e0:e1],
-                MULT,
-            )
-
-        for a in range(PASSES):
-            for s in range(len(STRETCHES[a])):
-                cast(a, s)
-                quantise(a, s)
-            if a < PASSES - 1:
-                pick_codes(a)
-        group_w(0, 1, "w_grouped0")
-        group_w(1, 3, "w_grouped1")
-        group_w(3, 5, "w_grouped3")
-        group_w(5, 6, "late_codes1")
-        nc.vector.tensor_copy(*interleave(w_grouped[0][:, N // 2 :, :], w_raw[0][:, :, N // 2 :]))
-        nc.scalar.copy(*interleave(w_grouped[0][:, : N // 2, :], w_raw[0][:, :, : N // 2]))
-        quantise_w(0, 1)
-        early_scales = held.tile([P, S - HALF], U8, name="early_scales", tag="early_scales", align_bytes=256)
-        nc.vector.tensor_copy(early_scales[:], scales[:].indirect(offsets[:, : (S - HALF) // 16]))
-        pick_last(0)
-        cast_w(1, nc.scalar.copy)
-        cast_w(2, nc.scalar.copy)
-        quantise_w(1, 3)
-        cast_w(3, nc.scalar.copy)
-        cast_w(4, nc.scalar.copy)
-        quantise_w(3, 5)
-        cast_w(5, nc.scalar.copy)
-        quantise_w(5, 6)
-        multiply(0)
-        late_scales = held.tile([P, HALF], U8, name="late_scales", tag="w_raw5", align_bytes=256)
-        nc.vector.tensor_copy(late_scales[:], scales[:].indirect(offsets[:, (S - HALF) // 16 :]))
-        pick_last(1)
-        multiply(1)
-        put_back(0, HALF, HALF)
-        put_back(HALF, S, 0)
-        nc.sync.dma_start(out, window[:])
+        gated = [held.tile([P, V], F32, name=f"gated{d}", align_bytes=256) for d in range(D)]
+        for d in range(D):
+            nc.vector.tensor_tensor(gated[d][:], acc[:], gates[:, d * V : (d + 1) * V], MULT)
+        nc.scalar.activation(windows[0][:].indirect(offsets[:, : V // 16]), gated[0][:], COPY)
+        nc.vector.tensor_copy(windows[1][:].indirect(offsets[:, V // 16 :]), gated[1][:])
+        for c0, c1 in STORES:
+            total = held.tile([P, c1 - c0], F32, name=f"total{c0}", align_bytes=256)
+            nc.vector.tensor_tensor(total[:], windows[0][:, c0:c1], windows[1][:, c0:c1], ADD)
+            nc.sync.dma_start(out[:, c0:c1], total[:])

@@ -19,7 +19,8 @@ P = 128
 PACK = 4
 PASSES = K // (P * PACK)
 X_LOADS = (((0, 2), (2, 4)), ((0, 2), (2, 4)), ((0, 2), (2, 3), (3, 4)))
-SCALAR_ENTRIES = ((512, 512, 512, 0), (512, 512, 512, 0), (512, 512, 0, 256))
+SCALAR_ENTRIES = ((512, 0, 512, 0), (512, 256, 512, 0), (512, 384, 0, 224))
+SCALAR_INTERLEAVES = (0, 128, 0)
 W_LOADS = ((0, 2), (2, 4), (4, 5), (5, 6))
 VECTOR_CASTS = (5,)
 STORES = ((0, 512), (512, 1024))
@@ -76,7 +77,10 @@ def tile_picked_tome_lin_none_sub_e_kernel(tc, xT, w, gate, offs, out):
             grouped = {}
             for d in range(D):
                 grouped[d] = held.tile([P, V, PACK], BF16, name=f"grouped{a}_{d}", align_bytes=256)
-                nc.vector.tensor_copy(*interleave(grouped[d][:], picked[:, :, d * V : (d + 1) * V]))
+                cut = SCALAR_INTERLEAVES[a] if d == 0 else 0
+                if cut > 0:
+                    nc.scalar.copy(*interleave(grouped[d][:, :cut, :], picked[:, :, :cut]))
+                nc.vector.tensor_copy(*interleave(grouped[d][:, cut:, :], picked[:, :, d * V + cut : (d + 1) * V]))
             for d in range(D):
                 codes[a, d] = held.tile([P, V], U32, name=f"codes{a}_{d}", align_bytes=256)
                 scales[a, d] = held.tile([P, V], U8, name=f"scales{a}_{d}", align_bytes=256)

@@ -19,9 +19,9 @@ P = 128
 PACK = 4
 PASSES = K // (P * PACK)
 X_LOADS = (((0, 2), (2, 4)), ((0, 2), (2, 4)), ((0, 2), (2, 3), (3, 4)))
-SCALAR_ENTRIES = ((512, 0, 512, 0), (512, 256, 512, 0), (512, 384, 0, 224))
+SCALAR_ENTRIES = ((512, 0, 512, 0), (512, 256, 512, 0), (512, 384, 0, 256))
 SCALAR_INTERLEAVES = (0, 128, 0)
-W_LOADS = ((0, 2), (2, 4), (4, 5), (5, 6))
+W_LOADS = tuple((u, u + 1) for u in range(D * PASSES))
 VECTOR_CASTS = (5,)
 STORES = ((0, 512), (512, 1024))
 

@@ -18,11 +18,10 @@ COPY = mybir.ActivationFunctionType.Copy
 P = 128
 PACK = 4
 PASSES = K // (P * PACK)
-X_LOADS = (((0, 2), (2, 4)), ((0, 2), (2, 4)), ((0, 2), (2, 3), (3, 4)))
-SCALAR_ENTRIES = ((512, 0, 512, 0), (512, 256, 512, 0), (512, 384, 0, 256))
-SCALAR_INTERLEAVES = (0, 128, 0)
+X_LOADS = (((0, 2), (2, 4)), ((0, 2), (2, 4)), ((0, 1), (1, 2), (2, 3), (3, 4)))
+SCALAR_ENTRIES = ((512, 0, 512, 0), (512, 384, 512, 0), (512, 512, 128, 256))
 W_LOADS = tuple((u, u + 1) for u in range(D * PASSES))
-VECTOR_CASTS = (5,)
+SCALAR_COLUMNS = (128, 128, 128, 128, 96, 0)
 STORES = ((0, 512), (512, 1024))
 
 
@@ -77,10 +76,7 @@ def tile_picked_tome_lin_none_sub_e_kernel(tc, xT, w, gate, offs, out):
             grouped = {}
             for d in range(D):
                 grouped[d] = held.tile([P, V, PACK], BF16, name=f"grouped{a}_{d}", align_bytes=256)
-                cut = SCALAR_INTERLEAVES[a] if d == 0 else 0
-                if cut > 0:
-                    nc.scalar.copy(*interleave(grouped[d][:, :cut, :], picked[:, :, :cut]))
-                nc.vector.tensor_copy(*interleave(grouped[d][:, cut:, :], picked[:, :, d * V + cut : (d + 1) * V]))
+                nc.vector.tensor_copy(*interleave(grouped[d][:], picked[:, :, d * V : (d + 1) * V]))
             for d in range(D):
                 codes[a, d] = held.tile([P, V], U32, name=f"codes{a}_{d}", align_bytes=256)
                 scales[a, d] = held.tile([P, V], U8, name=f"scales{a}_{d}", align_bytes=256)
@@ -96,8 +92,11 @@ def tile_picked_tome_lin_none_sub_e_kernel(tc, xT, w, gate, offs, out):
             w_codes = held.tile([P, (u1 - u0) * N], U32, name=f"w_codes{u0}", align_bytes=256)
             w_scales = held.tile([P, (u1 - u0) * N], U8, name=f"w_scales{u0}", align_bytes=256)
             for u in range(u0, u1):
-                copy = nc.vector.tensor_copy if u in VECTOR_CASTS else nc.scalar.copy
-                copy(*interleave(w_grouped[:, u - u0, :, :], w_raw[u]))
+                cut = SCALAR_COLUMNS[u]
+                if cut > 0:
+                    nc.scalar.copy(*interleave(w_grouped[:, u - u0, :cut, :], w_raw[u][:, :, :cut]))
+                if cut < N:
+                    nc.vector.tensor_copy(*interleave(w_grouped[:, u - u0, cut:, :], w_raw[u][:, :, cut:]))
             nc.vector.quantize_mx(
                 out=w_codes[:].bitcast(FP8X4),
                 scales=w_scales[:],

@@ -19,9 +19,9 @@ P = 128
 PACK = 4
 PASSES = K // (P * PACK)
 X_LOADS = (((0, 2), (2, 4)), ((0, 2), (2, 4)), ((0, 1), (1, 2), (2, 3), (3, 4)))
-SCALAR_ENTRIES = ((512, 0, 512, 0), (512, 384, 512, 0), (512, 512, 128, 256))
+SCALAR_ENTRIES = ((512, 0, 512, 0), (512, 384, 512, 0), (512, 512, 128, 128))
 W_LOADS = tuple((u, u + 1) for u in range(D * PASSES))
-SCALAR_COLUMNS = (128, 128, 128, 128, 96, 0)
+SCALAR_COLUMNS = (128, 128, 128, 128, 128, 0)
 STORES = ((0, 512), (512, 1024))
 
 
@@ -71,8 +71,12 @@ def tile_picked_tome_lin_none_sub_e_kernel(tc, xT, w, gate, offs, out):
                 cut = SCALAR_ENTRIES[a][j]
                 if cut > 0:
                     nc.scalar.activation(picked[:, j, :cut], planes[a, j].indirect(offsets[:, : cut // 16]), COPY)
-                if cut < S:
-                    nc.vector.tensor_copy(picked[:, j, cut:], planes[a, j].indirect(offsets[:, cut // 16 :]))
+                stops = (V, S) if (a, j) == (PASSES - 1, PACK - 1) else (S,)
+                for stop in stops:
+                    if cut < stop:
+                        looked_up = planes[a, j].indirect(offsets[:, cut // 16 : stop // 16])
+                        nc.vector.tensor_copy(picked[:, j, cut:stop], looked_up)
+                        cut = stop
             grouped = {}
             for d in range(D):
                 grouped[d] = held.tile([P, V, PACK], BF16, name=f"grouped{a}_{d}", align_bytes=256)

@@ -18,17 +18,20 @@ COPY = mybir.ActivationFunctionType.Copy
 P = 128
 PACK = 4
 PASSES = K // (P * PACK)
-X_LOADS = (((0, 2), (2, 4)), ((0, 2), (2, 4)), ((0, 1), (1, 2), (2, 3), (3, 4)))
-SCALAR_ENTRIES = ((512, 0, 512, 0), (512, 384, 512, 0), (512, 512, 128, 128))
-W_LOADS = tuple((u, u + 1) for u in range(D * PASSES))
-SCALAR_COLUMNS = (128, 128, 128, 128, 128, 0)
-STORES = ((0, 512), (512, 1024))
+UNITS = D * PASSES
+STRIPE = 16
+LAST = PASSES - 1
+
+PLANES_A_LOAD = (2, 2, 1)
+SCALAR_ENTRIES = ((S, 0, S, 0), (S, 384, S, 0), (S, S, 128))
+SCALAR_COLUMNS = (N // 2, N, N, N, N, 0)
+STORES = ((0, 256), (256, 640), (640, T))
 
 
 def interleave(dst, src):
     return (
-        dst.rearrange("p (c i) t -> p c t i", i=2),
-        src.rearrange("p t (c i) -> p c t i", i=2),
+        dst.rearrange("p (c i) j -> p c j i", i=2),
+        src.rearrange("p j (c i) -> p c j i", i=2),
     )
 
 
@@ -38,92 +41,102 @@ def tile_picked_tome_lin_none_sub_e_kernel(tc, xT, w, gate, offs, out):
         held = ctx.enter_context(tc.tile_pool(name="held", bufs=1))
         psum = ctx.enter_context(tc.psum_pool(name="psum", bufs=1))
 
-        offsets = held.tile([P, S // 16], U16, name="offsets")
+        offsets = held.tile([P, S // STRIPE], U16, name="offsets")
         windows = [held.tile([P, T], F32, name=f"window{d}", align_bytes=256) for d in range(D)]
         gates = held.tile([P, S], F32, name="gates", align_bytes=256)
+
+        def entries(e0, e1):
+            return offsets[:, e0 // STRIPE : e1 // STRIPE]
 
         planes = {}
         for a in range(PASSES):
             rows = xT[a * P * PACK : (a + 1) * P * PACK, :].rearrange("(p j) t -> p j t", j=PACK)
-            for j0, j1 in X_LOADS[a]:
-                tile = held.tile([P, j1 - j0, T], F32, name=f"raw{a}_{j0}", align_bytes=256)
-                nc.sync.dma_start(tile[:], rows[:, j0:j1, :])
-                for j in range(j0, j1):
-                    planes[a, j] = tile[:, j - j0, :]
+            count = PLANES_A_LOAD[a]
+            for j0 in range(0, PACK, count):
+                loaded = held.tile([P, count, T], F32, name=f"planes{a}_{j0}", align_bytes=256)
+                nc.sync.dma_start(loaded[:], rows[:, j0 : j0 + count, :])
+                for j in range(count):
+                    planes[a, j0 + j] = loaded[:, j, :]
                 if (a, j0) == (0, 0):
                     nc.sync.dma_start(offsets[:], offs)
         w_rows = w.rearrange("d k m -> (d k) m").rearrange("(u p j) m -> p u j m", p=P, j=PACK)
-        w_raw = {}
-        for u0, u1 in W_LOADS:
-            tile = held.tile([P, u1 - u0, PACK, N], F32, name=f"w_raw{u0}", align_bytes=256)
-            nc.sync.dma_start(tile[:], w_rows[:, u0:u1, :, :])
-            for u in range(u0, u1):
-                w_raw[u] = tile[:, u - u0, :, :]
+        w_raw = [held.tile([P, PACK, N], F32, name=f"w_raw{u}", align_bytes=256) for u in range(UNITS)]
+        for u in range(UNITS):
+            nc.sync.dma_start(w_raw[u][:], w_rows[:, u, :, :])
         nc.sync.dma_start(gates[:], gate)
 
         nc.gpsimd.memset(windows[1][:], 0.0)
         nc.scalar.copy(windows[0][:], windows[1][:])
 
-        codes, scales = {}, {}
+        w_grouped = [held.tile([P, N, PACK], BF16, name=f"w_grouped{u}", align_bytes=256) for u in range(UNITS)]
+
+        def round_weights(u):
+            cut = SCALAR_COLUMNS[u]
+            if cut > 0:
+                nc.scalar.copy(*interleave(w_grouped[u][:, :cut, :], w_raw[u][:, :, :cut]))
+            if cut < N:
+                nc.vector.tensor_copy(*interleave(w_grouped[u][:, cut:, :], w_raw[u][:, :, cut:]))
+
+        def quantise(grouped, name):
+            width = grouped.shape[1]
+            words = held.tile([P, width], U32, name=f"words_{name}", align_bytes=256)
+            scales = held.tile([P, width], U8, name=f"scales_{name}", align_bytes=256)
+            nc.vector.quantize_mx(
+                out=words[:].bitcast(FP8X4),
+                scales=scales[:],
+                in_=grouped[:].rearrange("p c j -> p (c j)"),
+            )
+            return words[:].bitcast(FP8X4), scales[:]
+
+        tokens = {}
         for a in range(PASSES):
             picked = held.tile([P, PACK, S], F32, name=f"picked{a}", align_bytes=256)
-            for j in range(PACK):
-                cut = SCALAR_ENTRIES[a][j]
-                if cut > 0:
-                    nc.scalar.activation(picked[:, j, :cut], planes[a, j].indirect(offsets[:, : cut // 16]), COPY)
-                stops = (V, S) if (a, j) == (PASSES - 1, PACK - 1) else (S,)
-                for stop in stops:
-                    if cut < stop:
-                        looked_up = planes[a, j].indirect(offsets[:, cut // 16 : stop // 16])
-                        nc.vector.tensor_copy(picked[:, j, cut:stop], looked_up)
-                        cut = stop
-            grouped = {}
-            for d in range(D):
-                grouped[d] = held.tile([P, V, PACK], BF16, name=f"grouped{a}_{d}", align_bytes=256)
-                nc.vector.tensor_copy(*interleave(grouped[d][:], picked[:, :, d * V : (d + 1) * V]))
-            for d in range(D):
-                codes[a, d] = held.tile([P, V], U32, name=f"codes{a}_{d}", align_bytes=256)
-                scales[a, d] = held.tile([P, V], U8, name=f"scales{a}_{d}", align_bytes=256)
-                nc.vector.quantize_mx(
-                    out=codes[a, d][:].bitcast(FP8X4),
-                    scales=scales[a, d][:],
-                    in_=grouped[d][:].rearrange("p t j -> p (t j)"),
-                )
 
-        acc = psum.tile([P, V], F32, name="acc")
-        for u0, u1 in W_LOADS:
-            w_grouped = held.tile([P, u1 - u0, N, PACK], BF16, name=f"w_grouped{u0}", align_bytes=256)
-            w_codes = held.tile([P, (u1 - u0) * N], U32, name=f"w_codes{u0}", align_bytes=256)
-            w_scales = held.tile([P, (u1 - u0) * N], U8, name=f"w_scales{u0}", align_bytes=256)
-            for u in range(u0, u1):
-                cut = SCALAR_COLUMNS[u]
+            def gathered(j, e0, e1):
+                return picked[:, j, e0:e1], planes[a, j].indirect(entries(e0, e1))
+
+            for j, cut in enumerate(SCALAR_ENTRIES[a]):
                 if cut > 0:
-                    nc.scalar.copy(*interleave(w_grouped[:, u - u0, :cut, :], w_raw[u][:, :, :cut]))
-                if cut < N:
-                    nc.vector.tensor_copy(*interleave(w_grouped[:, u - u0, cut:, :], w_raw[u][:, :, cut:]))
-            nc.vector.quantize_mx(
-                out=w_codes[:].bitcast(FP8X4),
-                scales=w_scales[:],
-                in_=w_grouped[:].rearrange("p u m j -> p (u m j)"),
+                    nc.scalar.activation(*gathered(j, 0, cut), COPY)
+                if cut < S:
+                    nc.vector.tensor_copy(*gathered(j, cut, S))
+            runs = [(0, V), (V, S)]
+            if a == LAST:
+                runs = [(0, V // 2), (V // 2, V), (V, S)]
+                nc.scalar.activation(*gathered(PACK - 1, V, S), COPY)
+                for e0, e1 in runs[:2]:
+                    nc.vector.tensor_copy(*gathered(PACK - 1, e0, e1))
+            grouped = [held.tile([P, V, PACK], BF16, name=f"grouped{a}_{d}", align_bytes=256) for d in range(D)]
+            for e0, e1 in runs:
+                d = e0 // V
+                nc.vector.tensor_copy(*interleave(grouped[d][:, e0 - d * V : e1 - d * V, :], picked[:, :, e0:e1]))
+            if a == LAST:
+                round_weights(0)
+            for d in range(D):
+                tokens[a, d] = quantise(grouped[d], f"x{a}_{d}")
+
+        sums = psum.tile([P, V], F32, name="sums")
+        for u in range(UNITS):
+            if u > 0:
+                round_weights(u)
+            w_words, w_scales = quantise(w_grouped[u], f"w{u}")
+            d, a = divmod(u, PASSES)
+            x_words, x_scales = tokens[a, d]
+            nc.tensor.matmul_mx(
+                out=sums[:],
+                lhsT=w_words,
+                lhsT_scale=w_scales,
+                rhs=x_words,
+                rhs_scale=x_scales,
+                start=(u == 0),
+                stop=(u == UNITS - 1),
             )
-            for u in range(u0, u1):
-                d, a = divmod(u, PASSES)
-                cols = slice((u - u0) * N, (u - u0 + 1) * N)
-                nc.tensor.matmul_mx(
-                    out=acc[:],
-                    lhsT=w_codes[:, cols].bitcast(FP8X4),
-                    lhsT_scale=w_scales[:, cols],
-                    rhs=codes[a, d][:].bitcast(FP8X4),
-                    rhs_scale=scales[a, d][:],
-                    start=(u == 0),
-                    stop=(u == D * PASSES - 1),
-                )
 
         gated = [held.tile([P, V], F32, name=f"gated{d}", align_bytes=256) for d in range(D)]
         for d in range(D):
-            nc.vector.tensor_tensor(gated[d][:], acc[:], gates[:, d * V : (d + 1) * V], MULT)
-        nc.scalar.activation(windows[0][:].indirect(offsets[:, : V // 16]), gated[0][:], COPY)
-        nc.vector.tensor_copy(windows[1][:].indirect(offsets[:, V // 16 :]), gated[1][:])
+            nc.vector.tensor_tensor(gated[d][:], sums[:], gates[:, d * V : (d + 1) * V], MULT)
+        nc.scalar.activation(windows[0][:].indirect(entries(0, V)), gated[0][:], COPY)
+        nc.vector.tensor_copy(windows[1][:].indirect(entries(V, S)), gated[1][:])
         for c0, c1 in STORES:
             total = held.tile([P, c1 - c0], F32, name=f"total{c0}", align_bytes=256)
             nc.vector.tensor_tensor(total[:], windows[0][:, c0:c1], windows[1][:, c0:c1], ADD)

@@ -25,7 +25,7 @@ LAST = PASSES - 1
 PLANES_A_LOAD = (2, 2, 1)
 SCALAR_ENTRIES = ((S, 0, S, 0), (S, 384, S, 0), (S, S, 128))
 SCALAR_COLUMNS = (N // 2, N, N, N, N, 0)
-STORES = ((0, 256), (256, 640), (640, T))
+STORES = ((0, T // 2), (T // 2, T))
 
 
 def interleave(dst, src):

@@ -24,7 +24,8 @@ LAST = PASSES - 1
 
 PLANES_A_LOAD = (2, 2, 1)
 SCALAR_ENTRIES = ((S, 0, S, 0), (S, 384, S, 0), (S, S, 128))
-SCALAR_COLUMNS = (N // 2, N, N, N, N, 0)
+UNITS_A_LOAD = (2, 2, 1, 1)
+SCALAR_UNITS = (0, 1, 2, 4)
 STORES = ((0, T // 2), (T // 2, T))
 
 
@@ -60,9 +61,12 @@ def tile_picked_tome_lin_none_sub_e_kernel(tc, xT, w, gate, offs, out):
                 if (a, j0) == (0, 0):
                     nc.sync.dma_start(offsets[:], offs)
         w_rows = w.rearrange("d k m -> (d k) m").rearrange("(u p j) m -> p u j m", p=P, j=PACK)
-        w_raw = [held.tile([P, PACK, N], F32, name=f"w_raw{u}", align_bytes=256) for u in range(UNITS)]
-        for u in range(UNITS):
-            nc.sync.dma_start(w_raw[u][:], w_rows[:, u, :, :])
+        w_raw = []
+        for count in UNITS_A_LOAD:
+            u0 = len(w_raw)
+            loaded = held.tile([P, count, PACK, N], F32, name=f"w_raw{u0}", align_bytes=256)
+            nc.sync.dma_start(loaded[:], w_rows[:, u0 : u0 + count, :, :])
+            w_raw.extend(loaded[:, i, :, :] for i in range(count))
         nc.sync.dma_start(gates[:], gate)
 
         nc.gpsimd.memset(windows[1][:], 0.0)
@@ -71,11 +75,10 @@ def tile_picked_tome_lin_none_sub_e_kernel(tc, xT, w, gate, offs, out):
         w_grouped = [held.tile([P, N, PACK], BF16, name=f"w_grouped{u}", align_bytes=256) for u in range(UNITS)]
 
         def round_weights(u):
-            cut = SCALAR_COLUMNS[u]
-            if cut > 0:
-                nc.scalar.copy(*interleave(w_grouped[u][:, :cut, :], w_raw[u][:, :, :cut]))
-            if cut < N:
-                nc.vector.tensor_copy(*interleave(w_grouped[u][:, cut:, :], w_raw[u][:, :, cut:]))
+            if u in SCALAR_UNITS:
+                nc.scalar.copy(*interleave(w_grouped[u][:], w_raw[u]))
+            else:
+                nc.vector.tensor_copy(*interleave(w_grouped[u][:], w_raw[u]))
 
         def quantise(grouped, name):
             width = grouped.shape[1]
@@ -110,15 +113,12 @@ def tile_picked_tome_lin_none_sub_e_kernel(tc, xT, w, gate, offs, out):
             for e0, e1 in runs:
                 d = e0 // V
                 nc.vector.tensor_copy(*interleave(grouped[d][:, e0 - d * V : e1 - d * V, :], picked[:, :, e0:e1]))
-            if a == LAST:
-                round_weights(0)
             for d in range(D):
                 tokens[a, d] = quantise(grouped[d], f"x{a}_{d}")
 
         sums = psum.tile([P, V], F32, name="sums")
         for u in range(UNITS):
-            if u > 0:
-                round_weights(u)
+            round_weights(u)
             w_words, w_scales = quantise(w_grouped[u], f"w{u}")
             d, a = divmod(u, PASSES)
             x_words, x_scales = tokens[a, d]

@@ -133,7 +133,7 @@ def tile_picked_tome_lin_none_sub_e_kernel(tc, xT, w, gate, offs, out):
             )
 
         gated = [held.tile([P, V], F32, name=f"gated{d}", align_bytes=256) for d in range(D)]
-        for d in range(D):
+        for d in (1, 0):
             nc.vector.tensor_tensor(gated[d][:], sums[:], gates[:, d * V : (d + 1) * V], MULT)
         nc.scalar.activation(windows[0][:].indirect(entries(0, V)), gated[0][:], COPY)
         nc.vector.tensor_copy(windows[1][:].indirect(entries(V, S)), gated[1][:])

@@ -103,16 +103,24 @@ def tile_picked_tome_lin_none_sub_e_kernel(tc, xT, w, gate, offs, out):
                     nc.scalar.activation(*gathered(j, 0, cut), COPY)
                 if cut < S:
                     nc.vector.tensor_copy(*gathered(j, cut, S))
-            runs = [(0, V), (V, S)]
-            if a == LAST:
-                runs = [(0, V // 2), (V // 2, V), (V, S)]
-                nc.scalar.activation(*gathered(PACK - 1, V, S), COPY)
-                for e0, e1 in runs[:2]:
-                    nc.vector.tensor_copy(*gathered(PACK - 1, e0, e1))
             grouped = [held.tile([P, V, PACK], BF16, name=f"grouped{a}_{d}", align_bytes=256) for d in range(D)]
-            for e0, e1 in runs:
+
+            def interleaved(e0, e1):
                 d = e0 // V
-                nc.vector.tensor_copy(*interleave(grouped[d][:, e0 - d * V : e1 - d * V, :], picked[:, :, e0:e1]))
+                return interleave(grouped[d][:, e0 - d * V : e1 - d * V, :], picked[:, :, e0:e1])
+
+            if a < LAST:
+                for d in range(D):
+                    nc.vector.tensor_copy(*interleaved(d * V, (d + 1) * V))
+            else:
+                runs = [(e0, e0 + S // 4) for e0 in range(0, S, S // 4)]
+                for run in (runs[3], runs[2]):
+                    nc.scalar.activation(*gathered(PACK - 1, *run), COPY)
+                for run in runs[:2]:
+                    nc.vector.tensor_copy(*gathered(PACK - 1, *run))
+                nc.scalar.copy(*interleaved(*runs[3]))
+                for run in runs[:3]:
+                    nc.vector.tensor_copy(*interleaved(*run))
             for d in range(D):
                 tokens[a, d] = quantise(grouped[d], f"x{a}_{d}")
 

@@ -25,7 +25,8 @@ LAST = PASSES - 1
 PLANES_A_LOAD = (2, 2, 1)
 SCALAR_ENTRIES = ((S, 0, S, 0), (S, 384, S, 0), (S, S, 128))
 UNITS_A_LOAD = (2, 2, 1, 1)
-SCALAR_UNITS = (0, 1, 2, 4)
+SCALAR_COLUMNS = (N, N, N, 0, N, N // 4)
+SCALAR_RUN = 96
 STORES = ((0, T // 2), (T // 2, T))
 
 
@@ -75,10 +76,11 @@ def tile_picked_tome_lin_none_sub_e_kernel(tc, xT, w, gate, offs, out):
         w_grouped = [held.tile([P, N, PACK], BF16, name=f"w_grouped{u}", align_bytes=256) for u in range(UNITS)]
 
         def round_weights(u):
-            if u in SCALAR_UNITS:
-                nc.scalar.copy(*interleave(w_grouped[u][:], w_raw[u]))
-            else:
-                nc.vector.tensor_copy(*interleave(w_grouped[u][:], w_raw[u]))
+            cut = SCALAR_COLUMNS[u]
+            if cut > 0:
+                nc.scalar.copy(*interleave(w_grouped[u][:, :cut, :], w_raw[u][:, :, :cut]))
+            if cut < N:
+                nc.vector.tensor_copy(*interleave(w_grouped[u][:, cut:, :], w_raw[u][:, :, cut:]))
 
         def quantise(grouped, name):
             width = grouped.shape[1]
@@ -113,7 +115,7 @@ def tile_picked_tome_lin_none_sub_e_kernel(tc, xT, w, gate, offs, out):
                 for d in range(D):
                     nc.vector.tensor_copy(*interleaved(d * V, (d + 1) * V))
             else:
-                runs = [(e0, e0 + S // 4) for e0 in range(0, S, S // 4)]
+                runs = [(0, V // 2), (V // 2, V), (V, S - SCALAR_RUN), (S - SCALAR_RUN, S)]
                 for run in (runs[3], runs[2]):
                     nc.scalar.activation(*gathered(PACK - 1, *run), COPY)
                 for run in runs[:2]:

@@ -23,7 +23,7 @@ STRIPE = 16
 LAST = PASSES - 1
 
 PLANES_A_LOAD = (2, 2, 1)
-SCALAR_ENTRIES = ((S, 0, S, 0), (S, 384, S, 0), (S, S, 128))
+SCALAR_ENTRIES = ((S, 0), (S, V), (S, S, 96))
 UNITS_A_LOAD = (2, 2, 1, 1)
 SCALAR_COLUMNS = (N, N, N, 0, N, N // 4)
 SCALAR_RUN = 96
@@ -112,6 +112,9 @@ def tile_picked_tome_lin_none_sub_e_kernel(tc, xT, w, gate, offs, out):
                 return interleave(grouped[d][:, e0 - d * V : e1 - d * V, :], picked[:, :, e0:e1])
 
             if a < LAST:
+                for d in range(D):
+                    nc.scalar.activation(*gathered(2, d * V, (d + 1) * V), COPY)
+                    nc.vector.tensor_copy(*gathered(3, d * V, (d + 1) * V))
                 for d in range(D):
                     nc.vector.tensor_copy(*interleaved(d * V, (d + 1) * V))
             else:

@@ -23,7 +23,7 @@ STRIPE = 16
 LAST = PASSES - 1
 
 PLANES_A_LOAD = (2, 2, 1)
-SCALAR_ENTRIES = ((S, 0), (S, V), (S, S, 96))
+SCALAR_ENTRIES = ((S, 0, S, 0), (S, V), (S, S, 96))
 UNITS_A_LOAD = (2, 2, 1, 1)
 SCALAR_COLUMNS = (N, N, N, 0, N, N // 4)
 SCALAR_RUN = 96
@@ -105,6 +105,13 @@ def tile_picked_tome_lin_none_sub_e_kernel(tc, xT, w, gate, offs, out):
                     nc.scalar.activation(*gathered(j, 0, cut), COPY)
                 if cut < S:
                     nc.vector.tensor_copy(*gathered(j, cut, S))
+            if a == 0:
+                both = held.tile([P, S, PACK], BF16, name="grouped0", align_bytes=256)
+                nc.vector.tensor_copy(*interleave(both[:], picked[:]))
+                words, scales = quantise(both, "x0")
+                for d in range(D):
+                    tokens[a, d] = words[:, d * V : (d + 1) * V], scales[:, d * V : (d + 1) * V]
+                continue
             grouped = [held.tile([P, V, PACK], BF16, name=f"grouped{a}_{d}", align_bytes=256) for d in range(D)]
 
             def interleaved(e0, e1):

@@ -23,9 +23,9 @@ STRIPE = 16
 LAST = PASSES - 1
 
 PLANES_A_LOAD = (2, 2, 1)
-SCALAR_ENTRIES = ((S, 0, S, 0), (S, V), (S, S, 96))
+SCALAR_ENTRIES = ((S, 0, S, 0), (S, V, S, 0), (S, S, 96))
 UNITS_A_LOAD = (2, 2, 1, 1)
-SCALAR_COLUMNS = (N, N, N, 0, N, N // 4)
+SCALAR_COLUMNS = (N, N, 3 * N // 4, 0, N, N // 2)
 SCALAR_RUN = 96
 STORES = ((0, T // 2), (T // 2, T))
 
@@ -82,15 +82,17 @@ def tile_picked_tome_lin_none_sub_e_kernel(tc, xT, w, gate, offs, out):
             if cut < N:
                 nc.vector.tensor_copy(*interleave(w_grouped[u][:, cut:, :], w_raw[u][:, :, cut:]))
 
-        def quantise(grouped, name):
+        def quantise(grouped, name, parts=1):
             width = grouped.shape[1]
             words = held.tile([P, width], U32, name=f"words_{name}", align_bytes=256)
             scales = held.tile([P, width], U8, name=f"scales_{name}", align_bytes=256)
-            nc.vector.quantize_mx(
-                out=words[:].bitcast(FP8X4),
-                scales=scales[:],
-                in_=grouped[:].rearrange("p c j -> p (c j)"),
-            )
+            for c0 in reversed(range(0, width, width // parts)):
+                cols = slice(c0, c0 + width // parts)
+                nc.vector.quantize_mx(
+                    out=words[:, cols].bitcast(FP8X4),
+                    scales=scales[:, cols],
+                    in_=grouped[:, cols, :].rearrange("p c j -> p (c j)"),
+                )
             return words[:].bitcast(FP8X4), scales[:]
 
         tokens = {}
@@ -120,9 +122,6 @@ def tile_picked_tome_lin_none_sub_e_kernel(tc, xT, w, gate, offs, out):
 
             if a < LAST:
                 for d in range(D):
-                    nc.scalar.activation(*gathered(2, d * V, (d + 1) * V), COPY)
-                    nc.vector.tensor_copy(*gathered(3, d * V, (d + 1) * V))
-                for d in range(D):
                     nc.vector.tensor_copy(*interleaved(d * V, (d + 1) * V))
             else:
                 runs = [(0, V // 2), (V // 2, V), (V, S - SCALAR_RUN), (S - SCALAR_RUN, S)]
@@ -139,7 +138,7 @@ def tile_picked_tome_lin_none_sub_e_kernel(tc, xT, w, gate, offs, out):
         sums = psum.tile([P, V], F32, name="sums")
         for u in range(UNITS):
             round_weights(u)
-            w_words, w_scales = quantise(w_grouped[u], f"w{u}")
+            w_words, w_scales = quantise(w_grouped[u], f"w{u}", 2 if u == UNITS - 1 else 1)
             d, a = divmod(u, PASSES)
             x_words, x_scales = tokens[a, d]
             nc.tensor.matmul_mx(

@@ -21,9 +21,10 @@ PASSES = K // (P * PACK)
 UNITS = D * PASSES
 STRIPE = 16
 LAST = PASSES - 1
+HALF = V // 2
 
 PLANES_A_LOAD = (2, 2, 1)
-SCALAR_ENTRIES = ((S, 0, S, 0), (S, V, S, 0), (S, S, 96))
+SCALAR_ENTRIES = ((S, S, S, 0), (S, 320, S, 0), (S, S, 96))
 UNITS_A_LOAD = (2, 2, 1, 1)
 SCALAR_COLUMNS = (N, N, 3 * N // 4, 0, N, N // 2)
 SCALAR_RUN = 96
@@ -135,27 +136,36 @@ def tile_picked_tome_lin_none_sub_e_kernel(tc, xT, w, gate, offs, out):
             for d in range(D):
                 tokens[a, d] = quantise(grouped[d], f"x{a}_{d}")
 
-        sums = psum.tile([P, V], F32, name="sums")
+        sums = [psum.tile([P, HALF], F32, name=f"sums{h}") for h in range(2)]
         for u in range(UNITS):
             round_weights(u)
             w_words, w_scales = quantise(w_grouped[u], f"w{u}", 2 if u == UNITS - 1 else 1)
             d, a = divmod(u, PASSES)
             x_words, x_scales = tokens[a, d]
-            nc.tensor.matmul_mx(
-                out=sums[:],
-                lhsT=w_words,
-                lhsT_scale=w_scales,
-                rhs=x_words,
-                rhs_scale=x_scales,
-                start=(u == 0),
-                stop=(u == UNITS - 1),
-            )
+            for h in range(2):
+                cols = slice(h * HALF, (h + 1) * HALF)
+                nc.tensor.matmul_mx(
+                    out=sums[h][:],
+                    lhsT=w_words,
+                    lhsT_scale=w_scales,
+                    rhs=x_words[:, cols],
+                    rhs_scale=x_scales[:, cols],
+                    start=(u == 0),
+                    stop=(u == UNITS - 1),
+                )
 
-        gated = [held.tile([P, V], F32, name=f"gated{d}", align_bytes=256) for d in range(D)]
+        gated = held.tile([P, S], F32, name="gated", align_bytes=256)
+        nc.vector.tensor_tensor(
+            gated[:].rearrange("p (d v) -> p d v", d=D)[:, :, :HALF],
+            sums[0][:].unsqueeze(1).to_broadcast([P, D, HALF]),
+            gates[:].rearrange("p (d v) -> p d v", d=D)[:, :, :HALF],
+            MULT,
+        )
         for d in (1, 0):
-            nc.vector.tensor_tensor(gated[d][:], sums[:], gates[:, d * V : (d + 1) * V], MULT)
-        nc.scalar.activation(windows[0][:].indirect(entries(0, V)), gated[0][:], COPY)
-        nc.vector.tensor_copy(windows[1][:].indirect(entries(V, S)), gated[1][:])
+            cols = slice(d * V + HALF, (d + 1) * V)
+            nc.vector.tensor_tensor(gated[:, cols], sums[1][:], gates[:, cols], MULT)
+        nc.scalar.activation(windows[0][:].indirect(entries(0, V)), gated[:, :V], COPY)
+        nc.vector.tensor_copy(windows[1][:].indirect(entries(V, S)), gated[:, V:])
         for c0, c1 in STORES:
             total = held.tile([P, c1 - c0], F32, name=f"total{c0}", align_bytes=256)
             nc.vector.tensor_tensor(total[:], windows[0][:, c0:c1], windows[1][:, c0:c1], ADD)

@@ -137,22 +137,30 @@ def tile_picked_tome_lin_none_sub_e_kernel(tc, xT, w, gate, offs, out):
                 tokens[a, d] = quantise(grouped[d], f"x{a}_{d}")
 
         sums = [psum.tile([P, HALF], F32, name=f"sums{h}") for h in range(2)]
-        for u in range(UNITS):
-            round_weights(u)
-            w_words, w_scales = quantise(w_grouped[u], f"w{u}", 2 if u == UNITS - 1 else 1)
+        weights = {}
+
+        def multiply(u, h):
             d, a = divmod(u, PASSES)
             x_words, x_scales = tokens[a, d]
-            for h in range(2):
-                cols = slice(h * HALF, (h + 1) * HALF)
-                nc.tensor.matmul_mx(
-                    out=sums[h][:],
-                    lhsT=w_words,
-                    lhsT_scale=w_scales,
-                    rhs=x_words[:, cols],
-                    rhs_scale=x_scales[:, cols],
-                    start=(u == 0),
-                    stop=(u == UNITS - 1),
-                )
+            cols = slice(h * HALF, (h + 1) * HALF)
+            nc.tensor.matmul_mx(
+                out=sums[h][:],
+                lhsT=weights[u][0],
+                lhsT_scale=weights[u][1],
+                rhs=x_words[:, cols],
+                rhs_scale=x_scales[:, cols],
+                start=(u == 0),
+                stop=(u == UNITS - 1 - h),
+            )
+
+        for u in range(UNITS):
+            round_weights(u)
+            weights[u] = quantise(w_grouped[u], f"w{u}", 2 if u == UNITS - 1 else 1)
+            multiply(u, 0)
+            if u < UNITS - 2:
+                multiply(u, 1)
+        for u in (UNITS - 1, UNITS - 2):
+            multiply(u, 1)
 
         gated = held.tile([P, S], F32, name="gated", align_bytes=256)
         nc.vector.tensor_tensor(

@@ -24,7 +24,7 @@ LAST = PASSES - 1
 HALF = V // 2
 
 PLANES_A_LOAD = (2, 2, 1)
-SCALAR_ENTRIES = ((S, S, S, 0), (S, 320, S, 0), (S, S, 96))
+SCALAR_ENTRIES = ((S, S, S, 0), (S, 320, S, 0), (S, S, 160))
 UNITS_A_LOAD = (2, 2, 1, 1)
 SCALAR_COLUMNS = (N, N, 3 * N // 4, 0, N, N // 2)
 SCALAR_RUN = 96

from contextlib import ExitStack

import concourse.mybir as mybir

K, T, D, S, V, N = 1536, 1024, 2, 512, 256, 128
FLOPS = 2 * K * D * V * N

F32 = mybir.dt.float32
BF16 = mybir.dt.bfloat16
U32 = mybir.dt.uint32
U16 = mybir.dt.uint16
U8 = mybir.dt.uint8
FP8X4 = mybir.dt.float8_e4m3fn_x4
MULT = mybir.AluOpType.mult
ADD = mybir.AluOpType.add
COPY = mybir.ActivationFunctionType.Copy

P = 128
PACK = 4
PASSES = K // (P * PACK)
UNITS = D * PASSES
STRIPE = 16
LAST = PASSES - 1
HALF = V // 2

PLANES_A_LOAD = (2, 2, 1)
SCALAR_ENTRIES = ((S, S, S, 0), (S, 320, S, 0), (S, S, 160))
UNITS_A_LOAD = (2, 2, 1, 1)
SCALAR_COLUMNS = (N, N, 3 * N // 4, 0, N, N // 2)
SCALAR_RUN = 96
STORES = ((0, T // 2), (T // 2, T))


def interleave(dst, src):
    return (
        dst.rearrange("p (c i) j -> p c j i", i=2),
        src.rearrange("p j (c i) -> p c j i", i=2),
    )


def tile_picked_tome_lin_none_sub_e_kernel(tc, xT, w, gate, offs, out):
    nc = tc.nc
    with ExitStack() as ctx:
        held = ctx.enter_context(tc.tile_pool(name="held", bufs=1))
        psum = ctx.enter_context(tc.psum_pool(name="psum", bufs=1))

        offsets = held.tile([P, S // STRIPE], U16, name="offsets")
        windows = [held.tile([P, T], F32, name=f"window{d}", align_bytes=256) for d in range(D)]
        gates = held.tile([P, S], F32, name="gates", align_bytes=256)

        def entries(e0, e1):
            return offsets[:, e0 // STRIPE : e1 // STRIPE]

        planes = {}
        for a in range(PASSES):
            rows = xT[a * P * PACK : (a + 1) * P * PACK, :].rearrange("(p j) t -> p j t", j=PACK)
            count = PLANES_A_LOAD[a]
            for j0 in range(0, PACK, count):
                loaded = held.tile([P, count, T], F32, name=f"planes{a}_{j0}", align_bytes=256)
                nc.sync.dma_start(loaded[:], rows[:, j0 : j0 + count, :])
                for j in range(count):
                    planes[a, j0 + j] = loaded[:, j, :]
                if (a, j0) == (0, 0):
                    nc.sync.dma_start(offsets[:], offs)
        w_rows = w.rearrange("d k m -> (d k) m").rearrange("(u p j) m -> p u j m", p=P, j=PACK)
        w_raw = []
        for count in UNITS_A_LOAD:
            u0 = len(w_raw)
            loaded = held.tile([P, count, PACK, N], F32, name=f"w_raw{u0}", align_bytes=256)
            nc.sync.dma_start(loaded[:], w_rows[:, u0 : u0 + count, :, :])
            w_raw.extend(loaded[:, i, :, :] for i in range(count))
        nc.sync.dma_start(gates[:], gate)

        nc.gpsimd.memset(windows[1][:], 0.0)
        nc.scalar.copy(windows[0][:], windows[1][:])

        w_grouped = [held.tile([P, N, PACK], BF16, name=f"w_grouped{u}", align_bytes=256) for u in range(UNITS)]

        def round_weights(u):
            cut = SCALAR_COLUMNS[u]
            if cut > 0:
                nc.scalar.copy(*interleave(w_grouped[u][:, :cut, :], w_raw[u][:, :, :cut]))
            if cut < N:
                nc.vector.tensor_copy(*interleave(w_grouped[u][:, cut:, :], w_raw[u][:, :, cut:]))

        def quantise(grouped, name, parts=1):
            width = grouped.shape[1]
            words = held.tile([P, width], U32, name=f"words_{name}", align_bytes=256)
            scales = held.tile([P, width], U8, name=f"scales_{name}", align_bytes=256)
            for c0 in reversed(range(0, width, width // parts)):
                cols = slice(c0, c0 + width // parts)
                nc.vector.quantize_mx(
                    out=words[:, cols].bitcast(FP8X4),
                    scales=scales[:, cols],
                    in_=grouped[:, cols, :].rearrange("p c j -> p (c j)"),
                )
            return words[:].bitcast(FP8X4), scales[:]

        tokens = {}
        for a in range(PASSES):
            picked = held.tile([P, PACK, S], F32, name=f"picked{a}", align_bytes=256)

            def gathered(j, e0, e1):
                return picked[:, j, e0:e1], planes[a, j].indirect(entries(e0, e1))

            for j, cut in enumerate(SCALAR_ENTRIES[a]):
                if cut > 0:
                    nc.scalar.activation(*gathered(j, 0, cut), COPY)
                if cut < S:
                    nc.vector.tensor_copy(*gathered(j, cut, S))
            if a == 0:
                both = held.tile([P, S, PACK], BF16, name="grouped0", align_bytes=256)
                nc.vector.tensor_copy(*interleave(both[:], picked[:]))
                words, scales = quantise(both, "x0")
                for d in range(D):
                    tokens[a, d] = words[:, d * V : (d + 1) * V], scales[:, d * V : (d + 1) * V]
                continue
            grouped = [held.tile([P, V, PACK], BF16, name=f"grouped{a}_{d}", align_bytes=256) for d in range(D)]

            def interleaved(e0, e1):
                d = e0 // V
                return interleave(grouped[d][:, e0 - d * V : e1 - d * V, :], picked[:, :, e0:e1])

            if a < LAST:
                for d in range(D):
                    nc.vector.tensor_copy(*interleaved(d * V, (d + 1) * V))
            else:
                runs = [(0, V // 2), (V // 2, V), (V, S - SCALAR_RUN), (S - SCALAR_RUN, S)]
                for run in (runs[3], runs[2]):
                    nc.scalar.activation(*gathered(PACK - 1, *run), COPY)
                for run in runs[:2]:
                    nc.vector.tensor_copy(*gathered(PACK - 1, *run))
                nc.scalar.copy(*interleaved(*runs[3]))
                for run in runs[:3]:
                    nc.vector.tensor_copy(*interleaved(*run))
            for d in range(D):
                tokens[a, d] = quantise(grouped[d], f"x{a}_{d}")

        sums = [psum.tile([P, HALF], F32, name=f"sums{h}") for h in range(2)]
        weights = {}

        def multiply(u, h):
            d, a = divmod(u, PASSES)
            x_words, x_scales = tokens[a, d]
            cols = slice(h * HALF, (h + 1) * HALF)
            nc.tensor.matmul_mx(
                out=sums[h][:],
                lhsT=weights[u][0],
                lhsT_scale=weights[u][1],
                rhs=x_words[:, cols],
                rhs_scale=x_scales[:, cols],
                start=(u == 0),
                stop=(u == UNITS - 1 - h),
            )

        for u in range(UNITS):
            round_weights(u)
            weights[u] = quantise(w_grouped[u], f"w{u}", 2 if u == UNITS - 1 else 1)
            multiply(u, 0)
            if u < UNITS - 2:
                multiply(u, 1)
        for u in (UNITS - 1, UNITS - 2):
            multiply(u, 1)

        gated = held.tile([P, S], F32, name="gated", align_bytes=256)
        nc.vector.tensor_tensor(
            gated[:].rearrange("p (d v) -> p d v", d=D)[:, :, :HALF],
            sums[0][:].unsqueeze(1).to_broadcast([P, D, HALF]),
            gates[:].rearrange("p (d v) -> p d v", d=D)[:, :, :HALF],
            MULT,
        )
        for d in (1, 0):
            cols = slice(d * V + HALF, (d + 1) * V)
            nc.vector.tensor_tensor(gated[:, cols], sums[1][:], gates[:, cols], MULT)
        nc.scalar.activation(windows[0][:].indirect(entries(0, V)), gated[:, :V], COPY)
        nc.vector.tensor_copy(windows[1][:].indirect(entries(V, S)), gated[:, V:])
        for c0, c1 in STORES:
            total = held.tile([P, c1 - c0], F32, name=f"total{c0}", align_bytes=256)
            nc.vector.tensor_tensor(total[:], windows[0][:, c0:c1], windows[1][:, c0:c1], ADD)
            nc.sync.dma_start(out[:, c0:c1], total[:])
